import numpy as np
import ml_dtypes


def mxq(x, axis, fmt="e4m3"):
    dtype, down = {"e4m3": (ml_dtypes.float8_e4m3fn, 7), "e5m2": (ml_dtypes.float8_e5m2, 14)}[fmt]
    v = np.moveaxis(np.asarray(x, np.float32).astype(ml_dtypes.bfloat16).astype(np.float64), axis, -1)
    blocks = v.reshape(v.shape[:-1] + (-1, 32))
    amax = np.abs(blocks).max(-1, keepdims=True)
    byte = np.maximum(np.where(amax > 0, np.frexp(amax)[1] - 1 + 127, 0) - down, 1)
    scale = np.exp2(byte - 127.0)
    codes = (blocks / scale).astype(np.float32).astype(dtype).astype(np.float64)
    return np.moveaxis((codes * scale).reshape(v.shape), -1, axis)


WIDE = False


def mx_kscale(k):
    if not WIDE:
        return np.ones(k)
    levels = np.array([10, -10, 5, -5, 0])
    if k % 512:
        return np.exp2(np.random.permutation(np.resize(levels, k // 32))).repeat(32)
    a = np.empty((k // 512, 16))
    for p in range(k // 512):
        a[p, :8] = np.random.permutation(np.resize(levels, 8))
        for g in range(8):
            far = levels[np.abs(levels - a[p, g]) >= 10]
            a[p, g + 8] = far[np.random.randint(len(far))]
    return np.exp2(a.ravel()).repeat(32)


def f64(x):
    return np.asarray(x).astype(np.float64)


def striped8(idx):
    return np.concatenate([x.reshape(-1, 16).T for x in idx]).astype(np.uint16)


def runs(offs, k):
    lists = np.stack([offs[16 * r : 16 * r + 16].T.reshape(-1) for r in range(8)]).astype(np.int64)
    return lists[np.arange(k) % 512 // 64]


def pack_weight(w):
    k, n = w.shape
    w = f64(np.asarray(w, np.float32).astype(ml_dtypes.bfloat16)).reshape(k // 32, 32, n)
    amax = np.abs(w).max(1)
    byte = np.clip(np.where(amax > 0, np.frexp(amax)[1] - 1 + 127 - 7, 1), 1, 254)
    scaled = (w * np.exp2(127.0 - byte)[:, None, :]).reshape(k, n).astype(np.float32)
    words = np.ascontiguousarray(scaled.reshape(k // 512, 128, 4, n).transpose(0, 1, 3, 2)).astype(ml_dtypes.float8_e4m3fn).view(np.uint8)
    return words, np.ascontiguousarray(byte.astype(np.uint8).reshape(k // 512, 16, n))


def unpack_weight(words, scales):
    g, p, n, _ = words.shape
    vals = np.ascontiguousarray(words).view(ml_dtypes.float8_e4m3fn).astype(np.float64) * np.repeat(np.exp2(scales.astype(np.float64) - 127.0), 8, axis=1)[..., None]
    return vals.transpose(0, 1, 3, 2).reshape(g * 512, n)


def relu(v):
    return np.maximum(v, 0.0)


K, T, S, N, H, U = 512, 2048, 512, 512, 512, 512


def setup_inputs():
    n = np.random.standard_normal
    s = mx_kscale(K)[:, None]
    u = mx_kscale(H)
    packed_xT = pack_weight(n((K, T)) * s)
    return {
        "x_words": packed_xT[0],
        "x_scales": packed_xT[1],
        "w1": (n((K, H)) / np.sqrt(K) / s).astype(np.float32),
        "len": np.random.uniform(0.5, 1.5, (H, U)).astype(np.float32),
        "idf": (np.random.uniform(0.5, 1.5, (H, 1)) * u[:, None]).astype(np.float32),
        "w2": (n((H, N)) / np.sqrt(H) / u[:, None]).astype(np.float32),
        "offs": striped8(np.stack([np.random.permutation(T)[:S] for _ in range(8)])),
        "doc": striped8(np.random.randint(0, U, (8, S))),
    }


def reference(x_words, x_scales, w1, len, idf, w2, offs, doc):
    xq = unpack_weight(x_words, x_scales)[np.arange(K)[:, None], runs(offs, K)]
    y = relu(mxq(f64(w1), 0, "e4m3").T @ xq)
    z = f64(idf) * ((2.0 * y) / (y + f64(len)[np.arange(H)[:, None], runs(doc, H)]))
    return mxq(f64(w2), 0, "e4m3").T @ mxq(z, 0, "e4m3")

@@ -1,0 +1,158 @@
+from contextlib import ExitStack
+
+import concourse.mybir as mybir
+
+K, T, S, N, H, U = 512, 2048, 512, 512, 512, 512
+FLOPS = 2 * K * H * S + 2 * H * N * S
+
+F32 = mybir.dt.float32
+BF16 = mybir.dt.bfloat16
+I32 = mybir.dt.int32
+U32 = mybir.dt.uint32
+U16 = mybir.dt.uint16
+U8 = mybir.dt.uint8
+FP8X4 = mybir.dt.float8_e4m3fn_x4
+ALU = mybir.AluOpType
+ACT = mybir.ActivationFunctionType
+
+P = 128
+PACK = 4
+CH = 128
+CHUNKS = S // CH
+HALF = S // 2
+PER_COL = 16
+
+
+def tile_picked_none_p_kernel(tc, x_words, x_scales, w1, len_, idf, w2, offs, doc, out):
+    nc = tc.nc
+    with ExitStack() as ctx:
+        keep = ctx.enter_context(tc.tile_pool(name="keep", bufs=1))
+        psum = ctx.enter_context(tc.psum_pool(name="psum", bufs=1))
+
+        offs_sb = keep.tile([P, S // PER_COL], U16, name="offs_sb")
+        doc_sb = keep.tile([P, S // PER_COL], U16, name="doc_sb")
+        nc.sync.dma_start(doc_sb[:], doc)
+        nc.sync.dma_start(offs_sb[:], offs)
+
+        warm = keep.tile([P, 2], F32, name="warm")
+        nc.vector.memset(warm[:, 0:1], 1.0)
+        nc.scalar.activation(warm[:, 1:2], warm[:, 0:1], ACT.Abs_reciprocal_sqrt)
+
+        sc_table = keep.tile([P, T], U8, name="sc_table", align_bytes=64)
+        nc.gpsimd.memset(sc_table[:].bitcast(I32), 0)
+        nc.scalar.dma_start(sc_table[0:P:8, :].bitcast(I32), x_scales[0].bitcast(I32))
+        x_sc = keep.tile([P, S], U8, name="x_sc", align_bytes=64)
+        nc.vector.memset(x_sc[:].bitcast(I32), 0)
+
+        len_rows = len_.rearrange("(p t) u -> p t u", t=PACK)
+        len_sb = [keep.tile([P, U], F32, name=f"len_sb{t}", align_bytes=64) for t in range(PACK)]
+        for t in range(PACK):
+            nc.sync.dma_start(len_sb[t][:], len_rows[:, t, :])
+
+        w1_rows = w1.rearrange("(p j) c -> p j c", j=PACK)
+        w1_raw = [keep.tile([P, PACK, H // 2], F32, name=f"w1_raw{h}", tag=f"raw{h}", align_bytes=64) for h in range(2)]
+        for h in range(2):
+            nc.sync.dma_start(w1_raw[h][:], w1_rows[:, :, h * (H // 2) : (h + 1) * (H // 2)])
+        word_table = keep.tile([P, T], U32, name="word_table", align_bytes=64)
+        nc.sync.dma_start(word_table[:].bitcast(I32), x_words[0].rearrange("p n r -> p (n r)").bitcast(I32))
+        idf_sb = keep.tile([P, PACK], F32, name="idf_sb")
+        nc.sync.dma_start(idf_sb[:], idf.rearrange("(p t) o -> p (t o)", t=PACK))
+
+        sc_picked = keep.tile([P, S], U8, name="sc_picked", align_bytes=64)
+        nc.vector.tensor_copy(sc_picked[:], sc_table[:].indirect(offs_sb[:]))
+        for e in range(4):
+            nc.scalar.dma_start(x_sc[e:P:32, :].bitcast(I32), sc_picked[8 * e : P : 32, :].bitcast(I32))
+
+        len_picked = keep.tile([P, PACK, S], F32, name="len_picked", align_bytes=64)
+        for t in range(PACK):
+            for h in range(2):
+                cols = slice(h * HALF // PER_COL, (h + 1) * HALF // PER_COL)
+                nc.vector.tensor_copy(len_picked[:, t, h * HALF : (h + 1) * HALF], len_sb[t][:].indirect(doc_sb[:, cols]))
+
+        w1_bf = keep.tile([P, PACK, P, PACK], BF16, name="w1_bf", align_bytes=64)
+        for h in range(2):
+            nc.scalar.copy(
+                w1_bf[:, :, h * (P // 2) : (h + 1) * (P // 2), :].rearrange("p t m j -> p m j t"),
+                w1_raw[h][:].rearrange("p j (m t) -> p m j t", t=PACK),
+            )
+        w2_rows = w2.rearrange("(p j) c -> p j c", j=PACK)
+        w2_raw = [keep.tile([P, PACK, N // 2], F32, name=f"w2_raw{h}", tag=f"raw{h}", align_bytes=64) for h in range(2)]
+        for h in range(2):
+            nc.sync.dma_start(w2_raw[h][:], w2_rows[:, :, h * (N // 2) : (h + 1) * (N // 2)])
+
+        w1_codes = keep.tile([P, H], U32, name="w1_codes", align_bytes=64)
+        w1_sc = keep.tile([P, H], U8, name="w1_sc", align_bytes=64)
+        nc.vector.quantize_mx(w1_codes[:].bitcast(FP8X4), w1_sc[:], w1_bf[:].rearrange("p t m j -> p (t m j)"))
+
+        x_codes = keep.tile([P, S], U32, name="x_codes", align_bytes=64)
+        for h in range(2):
+            cols = slice(h * HALF // PER_COL, (h + 1) * HALF // PER_COL)
+            nc.vector.tensor_copy(x_codes[:, h * HALF : (h + 1) * HALF], word_table[:].indirect(offs_sb[:, cols]))
+
+        idf4 = keep.tile([P, PACK], F32, name="idf4")
+        nc.scalar.mul(idf4[:], idf_sb[:], 4.0)
+
+        w2_bf = keep.tile([P, N, PACK], BF16, name="w2_bf", align_bytes=64)
+        for h in range(2):
+            nc.scalar.copy(
+                w2_bf[:, h * (N // 2) : (h + 1) * (N // 2), :].rearrange("p (c i) j -> p c j i", i=4),
+                w2_raw[h][:].rearrange("p j (c i) -> p c j i", i=4),
+            )
+        w2_codes = keep.tile([P, N], U32, name="w2_codes", align_bytes=64)
+        w2_sc = keep.tile([P, N], U8, name="w2_sc", align_bytes=64)
+        nc.vector.quantize_mx(w2_codes[:].bitcast(FP8X4), w2_sc[:], w2_bf[:].rearrange("p c j -> p (c j)"))
+
+        out_rows = out.rearrange("(b p) s -> p b s", p=P)
+        first = []
+        for c in range(CHUNKS):
+            places = slice(c * CH, (c + 1) * CH)
+            bank = psum.tile([P, PACK, CH], F32, name=f"first{c}")
+            for t in range(PACK):
+                feats = slice(t * P, (t + 1) * P)
+                nc.tensor.matmul_mx(
+                    bank[:, t, :],
+                    lhsT=w1_codes[:, feats].bitcast(FP8X4),
+                    lhsT_scale=w1_sc[:, feats],
+                    rhs=x_codes[:, places].bitcast(FP8X4),
+                    rhs_scale=x_sc[:, places],
+                    start=True,
+                    stop=True,
+                )
+            first.append(bank)
+
+        for c in range(CHUNKS):
+            places = slice(c * CH, (c + 1) * CH)
+            bank = first[c]
+            den = keep.tile([P, PACK, CH], F32, name=f"den{c}", align_bytes=64)
+            nc.vector.scalar_tensor_tensor(den[:], bank[:], 0.0, len_picked[:, :, places], ALU.max, ALU.add)
+            root = keep.tile([P, PACK, CH], F32, name=f"root{c}", align_bytes=64)
+            nc.scalar.activation(root[:], den[:], ACT.Abs_reciprocal_sqrt)
+            inv = keep.tile([P, PACK, CH], F32, name=f"inv{c}", align_bytes=64)
+            nc.scalar.activation(inv[:], root[:], ACT.Square)
+            half = keep.tile([P, PACK, CH], F32, name=f"half{c}", align_bytes=64)
+            nc.vector.tensor_scalar(half[:], den[:], 0.0, 0.5, ALU.is_ge, ALU.subtract)
+            fac = keep.tile([P, PACK, CH], F32, name=f"fac{c}", align_bytes=64)
+            for t in range(PACK):
+                nc.vector.scalar_tensor_tensor(fac[:, t, :], half[:, t, :], idf4[:, t : t + 1], inv[:, t, :], ALU.mult, ALU.mult)
+            z_bf = keep.tile([P, CH, PACK], BF16, name=f"z_bf{c}", align_bytes=64)
+            nc.vector.scalar_tensor_tensor(
+                z_bf[:], bank[:].rearrange("p t n -> p n t"), 0.0, fac[:].rearrange("p t n -> p n t"), ALU.max, ALU.mult
+            )
+            z_codes = keep.tile([P, CH], U32, name=f"z_codes{c}", align_bytes=64)
+            z_sc = keep.tile([P, CH], U8, name=f"z_sc{c}", align_bytes=64)
+            nc.vector.quantize_mx(z_codes[:].bitcast(FP8X4), z_sc[:], z_bf[:].rearrange("p n t -> p (n t)"))
+            second = psum.tile([P, N // P, CH], F32, name=f"second{c}")
+            for b in range(N // P):
+                rows = slice(b * P, (b + 1) * P)
+                nc.tensor.matmul_mx(
+                    second[:, b, :],
+                    lhsT=w2_codes[:, rows].bitcast(FP8X4),
+                    lhsT_scale=w2_sc[:, rows],
+                    rhs=z_codes[:].bitcast(FP8X4),
+                    rhs_scale=z_sc[:],
+                    start=True,
+                    stop=True,
+                )
+            res = keep.tile([P, N // P, CH], F32, name=f"res{c}", align_bytes=64)
+            nc.scalar.copy(res[:], second[:])
+            nc.sync.dma_start(out_rows[:, :, places], res[:])

@@ -17,142 +17,187 @@ ACT = mybir.ActivationFunctionType
 
 P = 128
 PACK = 4
-CH = 128
-CHUNKS = S // CH
-HALF = S // 2
+BLOCK_PARTS = 8
+QUADRANT = 32
 PER_COL = 16
+CHUNK = 128
+CHUNKS = S // CHUNK
+HALF = S // 2
+LINE = 4
 
 
-def tile_picked_none_p_kernel(tc, x_words, x_scales, w1, len_, idf, w2, offs, doc, out):
+def tile_picked_none_p_kernel(tc, x_words, x_scales, w1, lengths, idf, w2, offs, doc, out):
     nc = tc.nc
     with ExitStack() as ctx:
         keep = ctx.enter_context(tc.tile_pool(name="keep", bufs=1))
         psum = ctx.enter_context(tc.psum_pool(name="psum", bufs=1))
 
+        def half_of_list(list_tile, h):
+            return list_tile[:, h * HALF // PER_COL : (h + 1) * HALF // PER_COL]
+
         offs_sb = keep.tile([P, S // PER_COL], U16, name="offs_sb")
         doc_sb = keep.tile([P, S // PER_COL], U16, name="doc_sb")
         nc.sync.dma_start(doc_sb[:], doc)
-        nc.sync.dma_start(offs_sb[:], offs)
 
         warm = keep.tile([P, 2], F32, name="warm")
         nc.vector.memset(warm[:, 0:1], 1.0)
         nc.scalar.activation(warm[:, 1:2], warm[:, 0:1], ACT.Abs_reciprocal_sqrt)
 
-        sc_table = keep.tile([P, T], U8, name="sc_table", align_bytes=64)
-        nc.gpsimd.memset(sc_table[:].bitcast(I32), 0)
-        nc.scalar.dma_start(sc_table[0:P:8, :].bitcast(I32), x_scales[0].bitcast(I32))
-        x_sc = keep.tile([P, S], U8, name="x_sc", align_bytes=64)
-        nc.vector.memset(x_sc[:].bitcast(I32), 0)
+        scale_table = keep.tile([P, T], U8, name="scale_table", align_bytes=64)
+        nc.gpsimd.memset(scale_table[:].bitcast(I32), 0)
+        x_scale = keep.tile([P, S], U8, name="x_scale", align_bytes=64)
+        nc.vector.memset(x_scale[:].bitcast(I32), 0)
 
-        len_rows = len_.rearrange("(p t) u -> p t u", t=PACK)
-        len_sb = [keep.tile([P, U], F32, name=f"len_sb{t}", align_bytes=64) for t in range(PACK)]
-        for t in range(PACK):
+        len_rows = lengths.rearrange("(p t) u -> p t u", t=PACK)
+        len_sb = [keep.tile([P, U], F32, name=f"len_sb{t}", tag=f"len{t}", align_bytes=64) for t in range(PACK)]
+        nc.sync.dma_start(len_sb[0][:], len_rows[:, 0, :])
+        nc.sync.dma_start(offs_sb[:], offs)
+        nc.sync.dma_start(scale_table[0:P:BLOCK_PARTS, :].bitcast(I32), x_scales[0].bitcast(I32))
+        for t in range(1, PACK):
             nc.sync.dma_start(len_sb[t][:], len_rows[:, t, :])
-
-        w1_rows = w1.rearrange("(p j) c -> p j c", j=PACK)
-        w1_raw = [keep.tile([P, PACK, H // 2], F32, name=f"w1_raw{h}", tag=f"raw{h}", align_bytes=64) for h in range(2)]
-        for h in range(2):
-            nc.sync.dma_start(w1_raw[h][:], w1_rows[:, :, h * (H // 2) : (h + 1) * (H // 2)])
+        w1_raw = keep.tile([P, PACK, H], F32, name="w1_raw", align_bytes=64)
+        nc.sync.dma_start(w1_raw[:], w1.rearrange("(p j) c -> p j c", j=PACK))
         word_table = keep.tile([P, T], U32, name="word_table", align_bytes=64)
         nc.sync.dma_start(word_table[:].bitcast(I32), x_words[0].rearrange("p n r -> p (n r)").bitcast(I32))
-        idf_sb = keep.tile([P, PACK], F32, name="idf_sb")
-        nc.sync.dma_start(idf_sb[:], idf.rearrange("(p t) o -> p (t o)", t=PACK))
 
-        sc_picked = keep.tile([P, S], U8, name="sc_picked", align_bytes=64)
-        nc.vector.tensor_copy(sc_picked[:], sc_table[:].indirect(offs_sb[:]))
-        for e in range(4):
-            nc.scalar.dma_start(x_sc[e:P:32, :].bitcast(I32), sc_picked[8 * e : P : 32, :].bitcast(I32))
+        scale_picked = keep.tile([P, S], U8, name="scale_picked", align_bytes=64)
+        nc.vector.tensor_copy(scale_picked[:], scale_table[:].indirect(offs_sb[:]))
+        for e in range(QUADRANT // BLOCK_PARTS):
+            nc.scalar.dma_start(x_scale[e:P:QUADRANT, :].bitcast(I32), scale_picked[BLOCK_PARTS * e : P : QUADRANT, :].bitcast(I32))
 
         len_picked = keep.tile([P, PACK, S], F32, name="len_picked", align_bytes=64)
         for t in range(PACK):
             for h in range(2):
-                cols = slice(h * HALF // PER_COL, (h + 1) * HALF // PER_COL)
-                nc.vector.tensor_copy(len_picked[:, t, h * HALF : (h + 1) * HALF], len_sb[t][:].indirect(doc_sb[:, cols]))
+                nc.vector.tensor_copy(len_picked[:, t, h * HALF : (h + 1) * HALF], len_sb[t][:].indirect(half_of_list(doc_sb, h)))
 
-        w1_bf = keep.tile([P, PACK, P, PACK], BF16, name="w1_bf", align_bytes=64)
+        w1_bf = keep.tile([P, PACK, P, PACK], BF16, name="w1_bf", tag="w1_bf", align_bytes=64)
         for h in range(2):
             nc.scalar.copy(
                 w1_bf[:, :, h * (P // 2) : (h + 1) * (P // 2), :].rearrange("p t m j -> p m j t"),
-                w1_raw[h][:].rearrange("p j (m t) -> p m j t", t=PACK),
+                w1_raw[:, :, h * (H // 2) : (h + 1) * (H // 2)].rearrange("p j (m t) -> p m j t", t=PACK),
             )
-        w2_rows = w2.rearrange("(p j) c -> p j c", j=PACK)
-        w2_raw = [keep.tile([P, PACK, N // 2], F32, name=f"w2_raw{h}", tag=f"raw{h}", align_bytes=64) for h in range(2)]
-        for h in range(2):
-            nc.sync.dma_start(w2_raw[h][:], w2_rows[:, :, h * (N // 2) : (h + 1) * (N // 2)])
+
+        w2_raw = keep.tile([P, PACK, N], F32, name="w2_raw", tag="len1", align_bytes=64)
+        nc.sync.dma_start(w2_raw[:], w2.rearrange("(p j) c -> p j c", j=PACK))
+        idf_sb = keep.tile([P, PACK], F32, name="idf_sb")
+        nc.sync.dma_start(idf_sb[:], idf.rearrange("(p t) o -> p (t o)", t=PACK))
 
         w1_codes = keep.tile([P, H], U32, name="w1_codes", align_bytes=64)
-        w1_sc = keep.tile([P, H], U8, name="w1_sc", align_bytes=64)
-        nc.vector.quantize_mx(w1_codes[:].bitcast(FP8X4), w1_sc[:], w1_bf[:].rearrange("p t m j -> p (t m j)"))
+        w1_scale = keep.tile([P, H], U8, name="w1_scale", align_bytes=64)
+        nc.vector.quantize_mx(w1_codes[:].bitcast(FP8X4), w1_scale[:], w1_bf[:].rearrange("p t m j -> p (t m j)"))
 
-        x_codes = keep.tile([P, S], U32, name="x_codes", align_bytes=64)
-        for h in range(2):
-            cols = slice(h * HALF // PER_COL, (h + 1) * HALF // PER_COL)
-            nc.vector.tensor_copy(x_codes[:, h * HALF : (h + 1) * HALF], word_table[:].indirect(offs_sb[:, cols]))
+        x_codes = []
+        for h, tag in enumerate(("x_codes", "w1_bf")):
+            codes = keep.tile([P, HALF], U32, name=f"x_codes{h}", tag=tag, align_bytes=64)
+            nc.vector.tensor_copy(codes[:], word_table[:].indirect(half_of_list(offs_sb, h)))
+            x_codes.append(codes)
 
         idf4 = keep.tile([P, PACK], F32, name="idf4")
         nc.scalar.mul(idf4[:], idf_sb[:], 4.0)
 
         w2_bf = keep.tile([P, N, PACK], BF16, name="w2_bf", align_bytes=64)
         for h in range(2):
+            cols = slice(h * (N // 2), (h + 1) * (N // 2))
             nc.scalar.copy(
-                w2_bf[:, h * (N // 2) : (h + 1) * (N // 2), :].rearrange("p (c i) j -> p c j i", i=4),
-                w2_raw[h][:].rearrange("p j (c i) -> p c j i", i=4),
+                w2_bf[:, cols, :].rearrange("p (c i) j -> p c j i", i=LINE),
+                w2_raw[:, :, cols].rearrange("p j (c i) -> p c j i", i=LINE),
             )
         w2_codes = keep.tile([P, N], U32, name="w2_codes", align_bytes=64)
-        w2_sc = keep.tile([P, N], U8, name="w2_sc", align_bytes=64)
-        nc.vector.quantize_mx(w2_codes[:].bitcast(FP8X4), w2_sc[:], w2_bf[:].rearrange("p c j -> p (c j)"))
+        w2_scale = keep.tile([P, N], U8, name="w2_scale", align_bytes=64)
 
-        out_rows = out.rearrange("(b p) s -> p b s", p=P)
         first = []
         for c in range(CHUNKS):
-            places = slice(c * CH, (c + 1) * CH)
-            bank = psum.tile([P, PACK, CH], F32, name=f"first{c}")
+            h, start = divmod(c * CHUNK, HALF)
+            bank = psum.tile([P, PACK, CHUNK], F32, name=f"first{c}", tag=f"first{c}")
             for t in range(PACK):
                 feats = slice(t * P, (t + 1) * P)
                 nc.tensor.matmul_mx(
                     bank[:, t, :],
                     lhsT=w1_codes[:, feats].bitcast(FP8X4),
-                    lhsT_scale=w1_sc[:, feats],
-                    rhs=x_codes[:, places].bitcast(FP8X4),
-                    rhs_scale=x_sc[:, places],
+                    lhsT_scale=w1_scale[:, feats],
+                    rhs=x_codes[h][:, start : start + CHUNK].bitcast(FP8X4),
+                    rhs_scale=x_scale[:, c * CHUNK : (c + 1) * CHUNK],
                     start=True,
                     stop=True,
                 )
             first.append(bank)
 
-        for c in range(CHUNKS):
-            places = slice(c * CH, (c + 1) * CH)
-            bank = first[c]
-            den = keep.tile([P, PACK, CH], F32, name=f"den{c}", align_bytes=64)
-            nc.vector.scalar_tensor_tensor(den[:], bank[:], 0.0, len_picked[:, :, places], ALU.max, ALU.add)
-            root = keep.tile([P, PACK, CH], F32, name=f"root{c}", align_bytes=64)
-            nc.scalar.activation(root[:], den[:], ACT.Abs_reciprocal_sqrt)
-            inv = keep.tile([P, PACK, CH], F32, name=f"inv{c}", align_bytes=64)
-            nc.scalar.activation(inv[:], root[:], ACT.Square)
-            half = keep.tile([P, PACK, CH], F32, name=f"half{c}", align_bytes=64)
-            nc.vector.tensor_scalar(half[:], den[:], 0.0, 0.5, ALU.is_ge, ALU.subtract)
-            fac = keep.tile([P, PACK, CH], F32, name=f"fac{c}", align_bytes=64)
+        out_rows = out.rearrange("(b p) s -> p b s", p=P)
+        den, half_sign, inv_abs, factor, z_bf = {}, {}, {}, {}, {}
+
+        def make_denominator(c):
+            den[c] = keep.tile([P, PACK, CHUNK], F32, name=f"den{c}", align_bytes=64)
+            nc.vector.scalar_tensor_tensor(den[c][:], first[c][:], 0.0, len_picked[:, :, c * CHUNK : (c + 1) * CHUNK], ALU.max, ALU.add)
+            root = w2_raw[:, c, :]
+            nc.scalar.activation(root, den[c][:].rearrange("p t n -> p (t n)"), ACT.Abs_reciprocal_sqrt)
+            inv_abs[c] = keep.tile([P, PACK, CHUNK], F32, name=f"inv_abs{c}", align_bytes=64)
+            nc.scalar.activation(inv_abs[c][:].rearrange("p t n -> p (t n)"), root, ACT.Square)
+
+        def make_sign(c):
+            half_sign[c] = keep.tile([P, PACK, CHUNK], F32, name=f"half_sign{c}", align_bytes=64)
+            nc.vector.tensor_scalar(half_sign[c][:], den[c][:], 0.0, 0.5, ALU.is_ge, ALU.subtract)
+
+        def make_factor(c):
+            factor[c] = keep.tile([P, PACK, CHUNK], F32, name=f"factor{c}", align_bytes=64)
             for t in range(PACK):
-                nc.vector.scalar_tensor_tensor(fac[:, t, :], half[:, t, :], idf4[:, t : t + 1], inv[:, t, :], ALU.mult, ALU.mult)
-            z_bf = keep.tile([P, CH, PACK], BF16, name=f"z_bf{c}", align_bytes=64)
+                nc.vector.scalar_tensor_tensor(
+                    factor[c][:, t, :], half_sign[c][:, t, :], idf4[:, t : t + 1], inv_abs[c][:, t, :], ALU.mult, ALU.mult
+                )
+
+        def make_z(c):
+            z_bf[c] = keep.tile([P, CHUNK, PACK], BF16, name=f"z_bf{c}", align_bytes=64)
             nc.vector.scalar_tensor_tensor(
-                z_bf[:], bank[:].rearrange("p t n -> p n t"), 0.0, fac[:].rearrange("p t n -> p n t"), ALU.max, ALU.mult
+                z_bf[c][:], first[c][:].rearrange("p t n -> p n t"), 0.0, factor[c][:].rearrange("p t n -> p n t"), ALU.max, ALU.mult
             )
-            z_codes = keep.tile([P, CH], U32, name=f"z_codes{c}", align_bytes=64)
-            z_sc = keep.tile([P, CH], U8, name=f"z_sc{c}", align_bytes=64)
-            nc.vector.quantize_mx(z_codes[:].bitcast(FP8X4), z_sc[:], z_bf[:].rearrange("p n t -> p (n t)"))
-            second = psum.tile([P, N // P, CH], F32, name=f"second{c}")
-            for b in range(N // P):
+
+        def second_product(z_codes, z_scale, blocks, bank_tag):
+            bank = psum.tile([P, blocks.stop - blocks.start, CHUNK], F32, name=bank_tag, tag=bank_tag)
+            for b in blocks:
                 rows = slice(b * P, (b + 1) * P)
                 nc.tensor.matmul_mx(
-                    second[:, b, :],
+                    bank[:, b - blocks.start, :],
                     lhsT=w2_codes[:, rows].bitcast(FP8X4),
-                    lhsT_scale=w2_sc[:, rows],
+                    lhsT_scale=w2_scale[:, rows],
                     rhs=z_codes[:].bitcast(FP8X4),
-                    rhs_scale=z_sc[:],
+                    rhs_scale=z_scale[:],
                     start=True,
                     stop=True,
                 )
-            res = keep.tile([P, N // P, CH], F32, name=f"res{c}", align_bytes=64)
-            nc.scalar.copy(res[:], second[:])
-            nc.sync.dma_start(out_rows[:, :, places], res[:])
+            return bank
+
+        def project(c):
+            places = slice(c * CHUNK, (c + 1) * CHUNK)
+            z_codes = keep.tile([P, CHUNK], U32, name=f"z_codes{c}", align_bytes=64)
+            z_scale = keep.tile([P, CHUNK], U8, name=f"z_scale{c}", align_bytes=64)
+            nc.vector.quantize_mx(z_codes[:].bitcast(FP8X4), z_scale[:], z_bf[c][:].rearrange("p n t -> p (n t)"))
+            row_blocks = N // P
+            if c < CHUNKS - 1:
+                bank = second_product(z_codes, z_scale, range(row_blocks), f"second{c}")
+                result = keep.tile([P, row_blocks, CHUNK], F32, name=f"result{c}", align_bytes=64)
+                nc.scalar.copy(result[:], bank[:])
+                nc.sync.dma_start(out_rows[:, :, places], result[:])
+            else:
+                split = row_blocks // 2
+                bank = second_product(z_codes, z_scale, range(split), f"second{c}")
+                upper = keep.tile([P, split, CHUNK], F32, name="upper", align_bytes=64)
+                nc.scalar.copy(upper[:], bank[:])
+                nc.scalar.dma_start(out_rows[:, :split, places], upper[:])
+                bank = second_product(z_codes, z_scale, range(split, row_blocks), "first0")
+                lower = keep.tile([P, split, CHUNK], F32, name="lower", align_bytes=64)
+                nc.vector.tensor_copy(lower[:], bank[:])
+                nc.sync.dma_start(out_rows[:, split:, places], lower[:])
+
+        for c in range(CHUNKS + 1):
+            if c < CHUNKS:
+                make_denominator(c)
+            if c > 0:
+                make_sign(c - 1)
+        make_factor(0)
+        make_z(0)
+        for c in range(1, CHUNKS):
+            make_factor(c)
+            if c == 1:
+                nc.vector.quantize_mx(w2_codes[:].bitcast(FP8X4), w2_scale[:], w2_bf[:].rearrange("p c j -> p (c j)"))
+            project(c - 1)
+            make_z(c)
+        project(CHUNKS - 1)

@@ -23,6 +23,8 @@ PER_COL = 16
 CHUNK = 128
 CHUNKS = S // CHUNK
 HALF = S // 2
+GROUP = 16
+VECTOR_SIGNS = 2
 LINE = 4
 
 
@@ -53,17 +55,21 @@ def tile_picked_none_p_kernel(tc, x_words, x_scales, w1, lengths, idf, w2, offs,
         nc.sync.dma_start(len_sb[0][:], len_rows[:, 0, :])
         nc.sync.dma_start(offs_sb[:], offs)
         nc.sync.dma_start(scale_table[0:P:BLOCK_PARTS, :].bitcast(I32), x_scales[0].bitcast(I32))
-        for t in range(1, PACK):
-            nc.sync.dma_start(len_sb[t][:], len_rows[:, t, :])
+        nc.sync.dma_start(len_sb[1][:], len_rows[:, 1, :])
         w1_raw = keep.tile([P, PACK, H], F32, name="w1_raw", align_bytes=64)
         nc.sync.dma_start(w1_raw[:], w1.rearrange("(p j) c -> p j c", j=PACK))
+        for t in range(PACK // 2, PACK):
+            nc.sync.dma_start(len_sb[t][:], len_rows[:, t, :])
+        w2_rows = w2.rearrange("(p j) c -> p j c", j=PACK)
+        w2_raw = [keep.tile([P, PACK, N // 2], F32, name="w2_raw0", align_bytes=64)]
+        nc.sync.dma_start(w2_raw[0][:], w2_rows[:, :, : N // 2])
         word_table = keep.tile([P, T], U32, name="word_table", align_bytes=64)
         nc.sync.dma_start(word_table[:].bitcast(I32), x_words[0].rearrange("p n r -> p (n r)").bitcast(I32))
 
         scale_picked = keep.tile([P, S], U8, name="scale_picked", align_bytes=64)
         nc.vector.tensor_copy(scale_picked[:], scale_table[:].indirect(offs_sb[:]))
         for e in range(QUADRANT // BLOCK_PARTS):
-            nc.scalar.dma_start(x_scale[e:P:QUADRANT, :].bitcast(I32), scale_picked[BLOCK_PARTS * e : P : QUADRANT, :].bitcast(I32))
+            nc.sync.dma_start(x_scale[e:P:QUADRANT, :].bitcast(I32), scale_picked[BLOCK_PARTS * e : P : QUADRANT, :].bitcast(I32))
 
         len_picked = keep.tile([P, PACK, S], F32, name="len_picked", align_bytes=64)
         for t in range(PACK):
@@ -77,8 +83,8 @@ def tile_picked_none_p_kernel(tc, x_words, x_scales, w1, lengths, idf, w2, offs,
                 w1_raw[:, :, h * (H // 2) : (h + 1) * (H // 2)].rearrange("p j (m t) -> p m j t", t=PACK),
             )
 
-        w2_raw = keep.tile([P, PACK, N], F32, name="w2_raw", tag="len1", align_bytes=64)
-        nc.sync.dma_start(w2_raw[:], w2.rearrange("(p j) c -> p j c", j=PACK))
+        w2_raw.append(keep.tile([P, PACK, N // 2], F32, name="w2_raw1", tag="len2", align_bytes=64))
+        nc.sync.dma_start(w2_raw[1][:], w2_rows[:, :, N // 2 :])
         idf_sb = keep.tile([P, PACK], F32, name="idf_sb")
         nc.sync.dma_start(idf_sb[:], idf.rearrange("(p t) o -> p (t o)", t=PACK))
 
@@ -94,13 +100,15 @@ def tile_picked_none_p_kernel(tc, x_words, x_scales, w1, lengths, idf, w2, offs,
 
         idf4 = keep.tile([P, PACK], F32, name="idf4")
         nc.scalar.mul(idf4[:], idf_sb[:], 4.0)
+        idf2 = keep.tile([P, PACK], F32, name="idf2")
+        nc.scalar.mul(idf2[:], idf_sb[:], 2.0)
 
         w2_bf = keep.tile([P, N, PACK], BF16, name="w2_bf", align_bytes=64)
         for h in range(2):
             cols = slice(h * (N // 2), (h + 1) * (N // 2))
             nc.scalar.copy(
                 w2_bf[:, cols, :].rearrange("p (c i) j -> p c j i", i=LINE),
-                w2_raw[:, :, cols].rearrange("p j (c i) -> p c j i", i=LINE),
+                w2_raw[h][:].rearrange("p j (c i) -> p c j i", i=LINE),
             )
         w2_codes = keep.tile([P, N], U32, name="w2_codes", align_bytes=64)
         w2_scale = keep.tile([P, N], U8, name="w2_scale", align_bytes=64)
@@ -123,31 +131,42 @@ def tile_picked_none_p_kernel(tc, x_words, x_scales, w1, lengths, idf, w2, offs,
             first.append(bank)
 
         out_rows = out.rearrange("(b p) s -> p b s", p=P)
-        den, half_sign, inv_abs, factor, z_bf = {}, {}, {}, {}, {}
+        def halves(name):
+            return [keep.tile([P, PACK, HALF], F32, name=f"{name}{h}", align_bytes=64) for h in range(2)]
+
+        den, root, inv_abs, sign, factor = halves("den"), halves("root"), halves("inv_abs"), halves("sign"), halves("factor")
+        z_bf = {}
+
+        def of_chunk(tiles, c):
+            h, start = divmod(c * CHUNK, HALF)
+            return tiles[h][:, :, start : start + CHUNK]
 
         def make_denominator(c):
-            den[c] = keep.tile([P, PACK, CHUNK], F32, name=f"den{c}", align_bytes=64)
-            nc.vector.scalar_tensor_tensor(den[c][:], first[c][:], 0.0, len_picked[:, :, c * CHUNK : (c + 1) * CHUNK], ALU.max, ALU.add)
-            root = w2_raw[:, c, :]
-            nc.scalar.activation(root, den[c][:].rearrange("p t n -> p (t n)"), ACT.Abs_reciprocal_sqrt)
-            inv_abs[c] = keep.tile([P, PACK, CHUNK], F32, name=f"inv_abs{c}", align_bytes=64)
-            nc.scalar.activation(inv_abs[c][:].rearrange("p t n -> p (t n)"), root, ACT.Square)
+            nc.vector.scalar_tensor_tensor(of_chunk(den, c), first[c][:], 0.0, len_picked[:, :, c * CHUNK : (c + 1) * CHUNK], ALU.max, ALU.add)
+
+        def make_root(c):
+            nc.scalar.activation(of_chunk(root, c), of_chunk(den, c), ACT.Abs_reciprocal_sqrt)
+
+        def make_inverse(c):
+            nc.scalar.activation(of_chunk(inv_abs, c), of_chunk(root, c), ACT.Square)
 
         def make_sign(c):
-            half_sign[c] = keep.tile([P, PACK, CHUNK], F32, name=f"half_sign{c}", align_bytes=64)
-            nc.vector.tensor_scalar(half_sign[c][:], den[c][:], 0.0, 0.5, ALU.is_ge, ALU.subtract)
+            if c < VECTOR_SIGNS:
+                nc.vector.tensor_scalar(of_chunk(sign, c), of_chunk(den, c), 0.0, 0.5, ALU.is_ge, ALU.subtract)
+            else:
+                nc.scalar.activation(of_chunk(sign, c), of_chunk(den, c), ACT.Sign)
 
-        def make_factor(c):
-            factor[c] = keep.tile([P, PACK, CHUNK], F32, name=f"factor{c}", align_bytes=64)
+        def make_factor(h, places):
+            weight = idf4 if 2 * h < VECTOR_SIGNS else idf2
             for t in range(PACK):
                 nc.vector.scalar_tensor_tensor(
-                    factor[c][:, t, :], half_sign[c][:, t, :], idf4[:, t : t + 1], inv_abs[c][:, t, :], ALU.mult, ALU.mult
+                    factor[h][:, t, places], sign[h][:, t, places], weight[:, t : t + 1], inv_abs[h][:, t, places], ALU.mult, ALU.mult
                 )
 
         def make_z(c):
             z_bf[c] = keep.tile([P, CHUNK, PACK], BF16, name=f"z_bf{c}", align_bytes=64)
             nc.vector.scalar_tensor_tensor(
-                z_bf[c][:], first[c][:].rearrange("p t n -> p n t"), 0.0, factor[c][:].rearrange("p t n -> p n t"), ALU.max, ALU.mult
+                z_bf[c][:], first[c][:].rearrange("p t n -> p n t"), 0.0, of_chunk(factor, c).rearrange("p t n -> p n t"), ALU.max, ALU.mult
             )
 
         def second_product(z_codes, z_scale, blocks, bank_tag):
@@ -187,17 +206,29 @@ def tile_picked_none_p_kernel(tc, x_words, x_scales, w1, lengths, idf, w2, offs,
                 nc.vector.tensor_copy(lower[:], bank[:])
                 nc.sync.dma_start(out_rows[:, split:, places], lower[:])
 
-        for c in range(CHUNKS + 1):
-            if c < CHUNKS:
-                make_denominator(c)
-            if c > 0:
-                make_sign(c - 1)
-        make_factor(0)
+        make_denominator(0)
+        make_denominator(1)
+        make_root(0)
+        make_root(1)
+        make_inverse(0)
+        make_inverse(1)
+        make_denominator(2)
+        make_denominator(3)
+        make_sign(0)
+        make_sign(1)
+        for c in range(CHUNKS // 2, CHUNKS):
+            make_root(c)
+            make_sign(c)
+            make_inverse(c)
+        nc.vector.quantize_mx(w2_codes[:].bitcast(FP8X4), w2_scale[:], w2_bf[:].rearrange("p c j -> p (c j)"))
+        make_factor(0, slice(0, HALF))
         make_z(0)
-        for c in range(1, CHUNKS):
-            make_factor(c)
-            if c == 1:
-                nc.vector.quantize_mx(w2_codes[:].bitcast(FP8X4), w2_scale[:], w2_bf[:].rearrange("p c j -> p (c j)"))
-            project(c - 1)
-            make_z(c)
-        project(CHUNKS - 1)
+        make_z(1)
+        project(0)
+        make_factor(1, slice(0, CHUNK))
+        project(1)
+        make_z(2)
+        make_factor(1, slice(CHUNK, HALF))
+        project(2)
+        make_z(3)
+        project(3)

@@ -60,16 +60,13 @@ def tile_picked_none_p_kernel(tc, x_words, x_scales, w1, lengths, idf, w2, offs,
         nc.sync.dma_start(w1_raw[:], w1.rearrange("(p j) c -> p j c", j=PACK))
         for t in range(PACK // 2, PACK):
             nc.sync.dma_start(len_sb[t][:], len_rows[:, t, :])
-        w2_rows = w2.rearrange("(p j) c -> p j c", j=PACK)
-        w2_raw = [keep.tile([P, PACK, N // 2], F32, name="w2_raw0", align_bytes=64)]
-        nc.sync.dma_start(w2_raw[0][:], w2_rows[:, :, : N // 2])
         word_table = keep.tile([P, T], U32, name="word_table", align_bytes=64)
         nc.sync.dma_start(word_table[:].bitcast(I32), x_words[0].rearrange("p n r -> p (n r)").bitcast(I32))
 
         scale_picked = keep.tile([P, S], U8, name="scale_picked", align_bytes=64)
         nc.vector.tensor_copy(scale_picked[:], scale_table[:].indirect(offs_sb[:]))
         for e in range(QUADRANT // BLOCK_PARTS):
-            nc.sync.dma_start(x_scale[e:P:QUADRANT, :].bitcast(I32), scale_picked[BLOCK_PARTS * e : P : QUADRANT, :].bitcast(I32))
+            nc.scalar.dma_start(x_scale[e:P:QUADRANT, :].bitcast(I32), scale_picked[BLOCK_PARTS * e : P : QUADRANT, :].bitcast(I32))
 
         len_picked = keep.tile([P, PACK, S], F32, name="len_picked", align_bytes=64)
         for t in range(PACK):
@@ -83,8 +80,8 @@ def tile_picked_none_p_kernel(tc, x_words, x_scales, w1, lengths, idf, w2, offs,
                 w1_raw[:, :, h * (H // 2) : (h + 1) * (H // 2)].rearrange("p j (m t) -> p m j t", t=PACK),
             )
 
-        w2_raw.append(keep.tile([P, PACK, N // 2], F32, name="w2_raw1", tag="len2", align_bytes=64))
-        nc.sync.dma_start(w2_raw[1][:], w2_rows[:, :, N // 2 :])
+        w2_raw = keep.tile([P, PACK, N], F32, name="w2_raw", tag="len1", align_bytes=64)
+        nc.sync.dma_start(w2_raw[:], w2.rearrange("(p j) c -> p j c", j=PACK))
         idf_sb = keep.tile([P, PACK], F32, name="idf_sb")
         nc.sync.dma_start(idf_sb[:], idf.rearrange("(p t) o -> p (t o)", t=PACK))
 
@@ -104,12 +101,9 @@ def tile_picked_none_p_kernel(tc, x_words, x_scales, w1, lengths, idf, w2, offs,
         nc.scalar.mul(idf2[:], idf_sb[:], 2.0)
 
         w2_bf = keep.tile([P, N, PACK], BF16, name="w2_bf", align_bytes=64)
-        for h in range(2):
-            cols = slice(h * (N // 2), (h + 1) * (N // 2))
-            nc.scalar.copy(
-                w2_bf[:, cols, :].rearrange("p (c i) j -> p c j i", i=LINE),
-                w2_raw[h][:].rearrange("p j (c i) -> p c j i", i=LINE),
-            )
+        for q in range(4):
+            cols = slice(q * (N // 4), (q + 1) * (N // 4))
+            nc.gpsimd.tensor_scalar(w2_bf[:, cols, :], w2_raw[:, :, cols].rearrange("p j c -> p c j"), 1.0, 0.0, ALU.mult, ALU.add)
         w2_codes = keep.tile([P, N], U32, name="w2_codes", align_bytes=64)
         w2_scale = keep.tile([P, N], U8, name="w2_scale", align_bytes=64)
 
@@ -220,11 +214,12 @@ def tile_picked_none_p_kernel(tc, x_words, x_scales, w1, lengths, idf, w2, offs,
             make_root(c)
             make_sign(c)
             make_inverse(c)
+        make_factor(0, slice(0, CHUNK))
         nc.vector.quantize_mx(w2_codes[:].bitcast(FP8X4), w2_scale[:], w2_bf[:].rearrange("p c j -> p (c j)"))
-        make_factor(0, slice(0, HALF))
         make_z(0)
-        make_z(1)
+        make_factor(0, slice(CHUNK, HALF))
         project(0)
+        make_z(1)
         make_factor(1, slice(0, CHUNK))
         project(1)
         make_z(2)

@@ -25,6 +25,7 @@ CHUNKS = S // CHUNK
 HALF = S // 2
 GROUP = 16
 VECTOR_SIGNS = 2
+SCALAR_COLS = 256
 LINE = 4
 
 
@@ -32,6 +33,7 @@ def tile_picked_none_p_kernel(tc, x_words, x_scales, w1, lengths, idf, w2, offs,
     nc = tc.nc
     with ExitStack() as ctx:
         keep = ctx.enter_context(tc.tile_pool(name="keep", bufs=1))
+        shared = ctx.enter_context(tc.tile_pool(name="shared", bufs=1))
         psum = ctx.enter_context(tc.psum_pool(name="psum", bufs=1))
 
         def half_of_list(list_tile, h):
@@ -51,7 +53,9 @@ def tile_picked_none_p_kernel(tc, x_words, x_scales, w1, lengths, idf, w2, offs,
         nc.vector.memset(x_scale[:].bitcast(I32), 0)
 
         len_rows = lengths.rearrange("(p t) u -> p t u", t=PACK)
-        len_sb = [keep.tile([P, U], F32, name=f"len_sb{t}", tag=f"len{t}", align_bytes=64) for t in range(PACK)]
+        left_bytes = PACK * SCALAR_COLS * 4
+        len_sb = {t: keep.tile([P, U], F32, name=f"len_sb{t}", align_bytes=64) for t in range(PACK) if t != 1}
+        len_sb[1] = shared.tile([P, U], F32, name="len_sb1", align_bytes=64, offset=left_bytes - 2 * U)
         nc.sync.dma_start(len_sb[0][:], len_rows[:, 0, :])
         nc.sync.dma_start(offs_sb[:], offs)
         nc.sync.dma_start(scale_table[0:P:BLOCK_PARTS, :].bitcast(I32), x_scales[0].bitcast(I32))
@@ -80,8 +84,11 @@ def tile_picked_none_p_kernel(tc, x_words, x_scales, w1, lengths, idf, w2, offs,
                 w1_raw[:, :, h * (H // 2) : (h + 1) * (H // 2)].rearrange("p j (m t) -> p m j t", t=PACK),
             )
 
-        w2_raw = keep.tile([P, PACK, N], F32, name="w2_raw", tag="len1", align_bytes=64)
-        nc.sync.dma_start(w2_raw[:], w2.rearrange("(p j) c -> p j c", j=PACK))
+        w2_rows = w2.rearrange("(p j) c -> p j c", j=PACK)
+        w2_left = shared.tile([P, PACK, SCALAR_COLS], F32, name="w2_left", align_bytes=64, offset=0)
+        nc.sync.dma_start(w2_left[:], w2_rows[:, :, :SCALAR_COLS])
+        w2_right = shared.tile([P, PACK, N - SCALAR_COLS], F32, name="w2_right", align_bytes=64, offset=left_bytes)
+        nc.sync.dma_start(w2_right[:], w2_rows[:, :, SCALAR_COLS:])
         idf_sb = keep.tile([P, PACK], F32, name="idf_sb")
         nc.sync.dma_start(idf_sb[:], idf.rearrange("(p t) o -> p (t o)", t=PACK))
 
@@ -101,9 +108,19 @@ def tile_picked_none_p_kernel(tc, x_words, x_scales, w1, lengths, idf, w2, offs,
         nc.scalar.mul(idf2[:], idf_sb[:], 2.0)
 
         w2_bf = keep.tile([P, N, PACK], BF16, name="w2_bf", align_bytes=64)
-        for q in range(4):
-            cols = slice(q * (N // 4), (q + 1) * (N // 4))
-            nc.gpsimd.tensor_scalar(w2_bf[:, cols, :], w2_raw[:, :, cols].rearrange("p j c -> p c j"), 1.0, 0.0, ALU.mult, ALU.add)
+        nc.scalar.copy(
+            w2_bf[:, :SCALAR_COLS, :].rearrange("p (c i) j -> p c j i", i=LINE),
+            w2_left[:].rearrange("p j (c i) -> p c j i", i=LINE),
+        )
+        for start in range(0, N - SCALAR_COLS, P):
+            nc.gpsimd.tensor_scalar(
+                w2_bf[:, SCALAR_COLS + start : SCALAR_COLS + start + P, :],
+                w2_right[:, :, start : start + P].rearrange("p j c -> p c j"),
+                1.0,
+                0.0,
+                ALU.mult,
+                ALU.add,
+            )
         w2_codes = keep.tile([P, N], U32, name="w2_codes", align_bytes=64)
         w2_scale = keep.tile([P, N], U8, name="w2_scale", align_bytes=64)
 

@@ -24,7 +24,7 @@ CHUNK = 128
 CHUNKS = S // CHUNK
 HALF = S // 2
 GROUP = 16
-VECTOR_SIGNS = 2
+VECTOR_SIGNS = 1
 SCALAR_COLS = 256
 LINE = 4
 
@@ -41,7 +41,6 @@ def tile_picked_none_p_kernel(tc, x_words, x_scales, w1, lengths, idf, w2, offs,
 
         offs_sb = keep.tile([P, S // PER_COL], U16, name="offs_sb")
         doc_sb = keep.tile([P, S // PER_COL], U16, name="doc_sb")
-        nc.sync.dma_start(doc_sb[:], doc)
 
         warm = keep.tile([P, 2], F32, name="warm")
         nc.vector.memset(warm[:, 0:1], 1.0)
@@ -57,6 +56,7 @@ def tile_picked_none_p_kernel(tc, x_words, x_scales, w1, lengths, idf, w2, offs,
         len_sb = {t: keep.tile([P, U], F32, name=f"len_sb{t}", align_bytes=64) for t in range(PACK) if t != 1}
         len_sb[1] = shared.tile([P, U], F32, name="len_sb1", align_bytes=64, offset=left_bytes - 2 * U)
         nc.sync.dma_start(len_sb[0][:], len_rows[:, 0, :])
+        nc.sync.dma_start(doc_sb[:], doc)
         nc.sync.dma_start(offs_sb[:], offs)
         nc.sync.dma_start(scale_table[0:P:BLOCK_PARTS, :].bitcast(I32), x_scales[0].bitcast(I32))
         nc.sync.dma_start(len_sb[1][:], len_rows[:, 1, :])
@@ -167,11 +167,11 @@ def tile_picked_none_p_kernel(tc, x_words, x_scales, w1, lengths, idf, w2, offs,
             else:
                 nc.scalar.activation(of_chunk(sign, c), of_chunk(den, c), ACT.Sign)
 
-        def make_factor(h, places):
-            weight = idf4 if 2 * h < VECTOR_SIGNS else idf2
+        def make_factor(c):
+            weight = idf4 if c < VECTOR_SIGNS else idf2
             for t in range(PACK):
                 nc.vector.scalar_tensor_tensor(
-                    factor[h][:, t, places], sign[h][:, t, places], weight[:, t : t + 1], inv_abs[h][:, t, places], ALU.mult, ALU.mult
+                    of_chunk(factor, c)[:, t, :], of_chunk(sign, c)[:, t, :], weight[:, t : t + 1], of_chunk(inv_abs, c)[:, t, :], ALU.mult, ALU.mult
                 )
 
         def make_z(c):
@@ -222,25 +222,25 @@ def tile_picked_none_p_kernel(tc, x_words, x_scales, w1, lengths, idf, w2, offs,
         make_root(0)
         make_root(1)
         make_inverse(0)
+        make_sign(1)
         make_inverse(1)
         make_denominator(2)
         make_denominator(3)
         make_sign(0)
-        make_sign(1)
         for c in range(CHUNKS // 2, CHUNKS):
             make_root(c)
             make_sign(c)
             make_inverse(c)
-        make_factor(0, slice(0, CHUNK))
         nc.vector.quantize_mx(w2_codes[:].bitcast(FP8X4), w2_scale[:], w2_bf[:].rearrange("p c j -> p (c j)"))
+        make_factor(0)
         make_z(0)
-        make_factor(0, slice(CHUNK, HALF))
+        make_factor(1)
         project(0)
         make_z(1)
-        make_factor(1, slice(0, CHUNK))
+        make_factor(2)
         project(1)
         make_z(2)
-        make_factor(1, slice(CHUNK, HALF))
+        make_factor(3)
         project(2)
         make_z(3)
         project(3)

@@ -23,9 +23,10 @@ PER_COL = 16
 CHUNK = 128
 CHUNKS = S // CHUNK
 HALF = S // 2
-GROUP = 16
-VECTOR_SIGNS = 1
-SCALAR_COLS = 256
+W2_HALF = N // 2
+W2_PIECE = N // 4
+VECTOR_SIGN_CHUNK = 0
+F32_BYTES = 4
 LINE = 4
 
 
@@ -52,9 +53,9 @@ def tile_picked_none_p_kernel(tc, x_words, x_scales, w1, lengths, idf, w2, offs,
         nc.vector.memset(x_scale[:].bitcast(I32), 0)
 
         len_rows = lengths.rearrange("(p t) u -> p t u", t=PACK)
-        left_bytes = PACK * SCALAR_COLS * 4
+        w2_half_bytes = PACK * W2_HALF * F32_BYTES
         len_sb = {t: keep.tile([P, U], F32, name=f"len_sb{t}", align_bytes=64) for t in range(PACK) if t != 1}
-        len_sb[1] = shared.tile([P, U], F32, name="len_sb1", align_bytes=64, offset=left_bytes - 2 * U)
+        len_sb[1] = shared.tile([P, U], F32, name="len_sb1", align_bytes=64, offset=w2_half_bytes - U * F32_BYTES // 2)
         nc.sync.dma_start(len_sb[0][:], len_rows[:, 0, :])
         nc.sync.dma_start(doc_sb[:], doc)
         nc.sync.dma_start(offs_sb[:], offs)
@@ -64,7 +65,7 @@ def tile_picked_none_p_kernel(tc, x_words, x_scales, w1, lengths, idf, w2, offs,
         nc.sync.dma_start(w1_raw[:], w1.rearrange("(p j) c -> p j c", j=PACK))
         for t in range(PACK // 2, PACK):
             nc.sync.dma_start(len_sb[t][:], len_rows[:, t, :])
-        word_table = keep.tile([P, T], U32, name="word_table", align_bytes=64)
+        word_table = keep.tile([P, T], U32, name="word_table", tag="word_table", align_bytes=64)
         nc.sync.dma_start(word_table[:].bitcast(I32), x_words[0].rearrange("p n r -> p (n r)").bitcast(I32))
 
         scale_picked = keep.tile([P, S], U8, name="scale_picked", align_bytes=64)
@@ -85,10 +86,11 @@ def tile_picked_none_p_kernel(tc, x_words, x_scales, w1, lengths, idf, w2, offs,
             )
 
         w2_rows = w2.rearrange("(p j) c -> p j c", j=PACK)
-        w2_left = shared.tile([P, PACK, SCALAR_COLS], F32, name="w2_left", align_bytes=64, offset=0)
-        nc.sync.dma_start(w2_left[:], w2_rows[:, :, :SCALAR_COLS])
-        w2_right = shared.tile([P, PACK, N - SCALAR_COLS], F32, name="w2_right", align_bytes=64, offset=left_bytes)
-        nc.sync.dma_start(w2_right[:], w2_rows[:, :, SCALAR_COLS:])
+        w2_raw = []
+        for h in range(2):
+            raw = shared.tile([P, PACK, W2_HALF], F32, name=f"w2_raw{h}", align_bytes=64, offset=h * w2_half_bytes)
+            nc.sync.dma_start(raw[:], w2_rows[:, :, h * W2_HALF : (h + 1) * W2_HALF])
+            w2_raw.append(raw)
         idf_sb = keep.tile([P, PACK], F32, name="idf_sb")
         nc.sync.dma_start(idf_sb[:], idf.rearrange("(p t) o -> p (t o)", t=PACK))
 
@@ -107,20 +109,15 @@ def tile_picked_none_p_kernel(tc, x_words, x_scales, w1, lengths, idf, w2, offs,
         idf2 = keep.tile([P, PACK], F32, name="idf2")
         nc.scalar.mul(idf2[:], idf_sb[:], 2.0)
 
-        w2_bf = keep.tile([P, N, PACK], BF16, name="w2_bf", align_bytes=64)
+        w2_bf = keep.tile([P, N, PACK], BF16, name="w2_bf", tag="word_table", align_bytes=64)
         nc.scalar.copy(
-            w2_bf[:, :SCALAR_COLS, :].rearrange("p (c i) j -> p c j i", i=LINE),
-            w2_left[:].rearrange("p j (c i) -> p c j i", i=LINE),
+            w2_bf[:, :W2_PIECE, :].rearrange("p (c i) j -> p c j i", i=LINE),
+            w2_raw[0][:, :, :W2_PIECE].rearrange("p j (c i) -> p c j i", i=LINE),
         )
-        for start in range(0, N - SCALAR_COLS, P):
-            nc.gpsimd.tensor_scalar(
-                w2_bf[:, SCALAR_COLS + start : SCALAR_COLS + start + P, :],
-                w2_right[:, :, start : start + P].rearrange("p j c -> p c j"),
-                1.0,
-                0.0,
-                ALU.mult,
-                ALU.add,
-            )
+        for col in range(W2_PIECE, N, W2_PIECE):
+            h, start = divmod(col, W2_HALF)
+            piece = w2_raw[h][:, :, start : start + W2_PIECE].rearrange("p j c -> p c j")
+            nc.gpsimd.tensor_scalar(w2_bf[:, col : col + W2_PIECE, :], piece, 1.0, 0.0, ALU.mult, ALU.add)
         w2_codes = keep.tile([P, N], U32, name="w2_codes", align_bytes=64)
         w2_scale = keep.tile([P, N], U8, name="w2_scale", align_bytes=64)
 
@@ -142,42 +139,42 @@ def tile_picked_none_p_kernel(tc, x_words, x_scales, w1, lengths, idf, w2, offs,
             first.append(bank)
 
         out_rows = out.rearrange("(b p) s -> p b s", p=P)
-        def halves(name):
-            return [keep.tile([P, PACK, HALF], F32, name=f"{name}{h}", align_bytes=64) for h in range(2)]
 
-        den, root, inv_abs, sign, factor = halves("den"), halves("root"), halves("inv_abs"), halves("sign"), halves("factor")
-        z_bf = {}
+        def per_chunk(name):
+            return [keep.tile([P, PACK, CHUNK], F32, name=f"{name}{c}", align_bytes=64) for c in range(CHUNKS)]
 
-        def of_chunk(tiles, c):
-            h, start = divmod(c * CHUNK, HALF)
-            return tiles[h][:, :, start : start + CHUNK]
+        den, root, inv_abs, sign, factor = (per_chunk(name) for name in ("den", "root", "inv_abs", "sign", "factor"))
+        z_bf = [keep.tile([P, CHUNK, PACK], BF16, name=f"z_bf{c}", align_bytes=64) for c in range(CHUNKS)]
+
+        def quantise_w2(h):
+            cols = slice(h * W2_HALF, (h + 1) * W2_HALF)
+            nc.vector.quantize_mx(w2_codes[:, cols].bitcast(FP8X4), w2_scale[:, cols], w2_bf[:, cols, :].rearrange("p c j -> p (c j)"))
 
         def make_denominator(c):
-            nc.vector.scalar_tensor_tensor(of_chunk(den, c), first[c][:], 0.0, len_picked[:, :, c * CHUNK : (c + 1) * CHUNK], ALU.max, ALU.add)
+            nc.vector.scalar_tensor_tensor(den[c][:], first[c][:], 0.0, len_picked[:, :, c * CHUNK : (c + 1) * CHUNK], ALU.max, ALU.add)
 
         def make_root(c):
-            nc.scalar.activation(of_chunk(root, c), of_chunk(den, c), ACT.Abs_reciprocal_sqrt)
+            nc.scalar.activation(root[c][:], den[c][:], ACT.Abs_reciprocal_sqrt)
 
         def make_inverse(c):
-            nc.scalar.activation(of_chunk(inv_abs, c), of_chunk(root, c), ACT.Square)
+            nc.scalar.activation(inv_abs[c][:], root[c][:], ACT.Square)
 
         def make_sign(c):
-            if c < VECTOR_SIGNS:
-                nc.vector.tensor_scalar(of_chunk(sign, c), of_chunk(den, c), 0.0, 0.5, ALU.is_ge, ALU.subtract)
+            if c == VECTOR_SIGN_CHUNK:
+                nc.vector.tensor_scalar(sign[c][:], den[c][:], 0.0, 0.5, ALU.is_ge, ALU.subtract)
             else:
-                nc.scalar.activation(of_chunk(sign, c), of_chunk(den, c), ACT.Sign)
+                nc.scalar.activation(sign[c][:], den[c][:], ACT.Sign)
 
         def make_factor(c):
-            weight = idf4 if c < VECTOR_SIGNS else idf2
+            weight = idf4 if c == VECTOR_SIGN_CHUNK else idf2
             for t in range(PACK):
                 nc.vector.scalar_tensor_tensor(
-                    of_chunk(factor, c)[:, t, :], of_chunk(sign, c)[:, t, :], weight[:, t : t + 1], of_chunk(inv_abs, c)[:, t, :], ALU.mult, ALU.mult
+                    factor[c][:, t, :], sign[c][:, t, :], weight[:, t : t + 1], inv_abs[c][:, t, :], ALU.mult, ALU.mult
                 )
 
         def make_z(c):
-            z_bf[c] = keep.tile([P, CHUNK, PACK], BF16, name=f"z_bf{c}", align_bytes=64)
             nc.vector.scalar_tensor_tensor(
-                z_bf[c][:], first[c][:].rearrange("p t n -> p n t"), 0.0, of_chunk(factor, c).rearrange("p t n -> p n t"), ALU.max, ALU.mult
+                z_bf[c][:], first[c][:].rearrange("p t n -> p n t"), 0.0, factor[c][:].rearrange("p t n -> p n t"), ALU.max, ALU.mult
             )
 
         def second_product(z_codes, z_scale, blocks, bank_tag):
@@ -227,20 +224,17 @@ def tile_picked_none_p_kernel(tc, x_words, x_scales, w1, lengths, idf, w2, offs,
         make_denominator(2)
         make_denominator(3)
         make_sign(0)
-        for c in range(CHUNKS // 2, CHUNKS):
+        for c in range(2, CHUNKS):
             make_root(c)
             make_sign(c)
             make_inverse(c)
-        nc.vector.quantize_mx(w2_codes[:].bitcast(FP8X4), w2_scale[:], w2_bf[:].rearrange("p c j -> p (c j)"))
+
+        quantise_w2(0)
         make_factor(0)
+        quantise_w2(1)
         make_z(0)
-        make_factor(1)
-        project(0)
-        make_z(1)
-        make_factor(2)
-        project(1)
-        make_z(2)
-        make_factor(3)
-        project(2)
-        make_z(3)
-        project(3)
+        for c in range(1, CHUNKS):
+            make_factor(c)
+            project(c - 1)
+            make_z(c)
+        project(CHUNKS - 1)

@@ -1,3 +1,4 @@
+import math
 from contextlib import ExitStack
 
 import concourse.mybir as mybir
@@ -22,6 +23,7 @@ QUADRANT = 32
 PER_COL = 16
 CHUNK = 128
 CHUNKS = S // CHUNK
+ROW_BLOCKS = N // P
 HALF = S // 2
 W2_HALF = N // 2
 W2_PIECE = N // 4
@@ -48,9 +50,9 @@ def tile_picked_none_p_kernel(tc, x_words, x_scales, w1, lengths, idf, w2, offs,
         nc.scalar.activation(warm[:, 1:2], warm[:, 0:1], ACT.Abs_reciprocal_sqrt)
 
         scale_table = keep.tile([P, T], U8, name="scale_table", align_bytes=64)
-        nc.gpsimd.memset(scale_table[:].bitcast(I32), 0)
+        nc.vector.memset(scale_table[:].bitcast(I32), 0)
         x_scale = keep.tile([P, S], U8, name="x_scale", align_bytes=64)
-        nc.vector.memset(x_scale[:].bitcast(I32), 0)
+        nc.gpsimd.memset(x_scale[:].bitcast(I32), 0)
 
         len_rows = lengths.rearrange("(p t) u -> p t u", t=PACK)
         w2_half_bytes = PACK * W2_HALF * F32_BYTES
@@ -104,11 +106,6 @@ def tile_picked_none_p_kernel(tc, x_words, x_scales, w1, lengths, idf, w2, offs,
             nc.vector.tensor_copy(codes[:], word_table[:].indirect(half_of_list(offs_sb, h)))
             x_codes.append(codes)
 
-        idf4 = keep.tile([P, PACK], F32, name="idf4")
-        nc.scalar.mul(idf4[:], idf_sb[:], 4.0)
-        idf2 = keep.tile([P, PACK], F32, name="idf2")
-        nc.scalar.mul(idf2[:], idf_sb[:], 2.0)
-
         w2_bf = keep.tile([P, N, PACK], BF16, name="w2_bf", tag="word_table", align_bytes=64)
         nc.scalar.copy(
             w2_bf[:, :W2_PIECE, :].rearrange("p (c i) j -> p c j i", i=LINE),
@@ -157,7 +154,8 @@ def tile_picked_none_p_kernel(tc, x_words, x_scales, w1, lengths, idf, w2, offs,
             nc.scalar.activation(root[c][:], den[c][:], ACT.Abs_reciprocal_sqrt)
 
         def make_inverse(c):
-            nc.scalar.activation(inv_abs[c][:], root[c][:], ACT.Square)
+            gain = 4.0 if c == VECTOR_SIGN_CHUNK else 2.0
+            nc.scalar.activation(inv_abs[c][:], root[c][:], ACT.Square, scale=math.sqrt(gain))
 
         def make_sign(c):
             if c == VECTOR_SIGN_CHUNK:
@@ -166,10 +164,9 @@ def tile_picked_none_p_kernel(tc, x_words, x_scales, w1, lengths, idf, w2, offs,
                 nc.scalar.activation(sign[c][:], den[c][:], ACT.Sign)
 
         def make_factor(c):
-            weight = idf4 if c == VECTOR_SIGN_CHUNK else idf2
             for t in range(PACK):
                 nc.vector.scalar_tensor_tensor(
-                    factor[c][:, t, :], sign[c][:, t, :], weight[:, t : t + 1], inv_abs[c][:, t, :], ALU.mult, ALU.mult
+                    factor[c][:, t, :], sign[c][:, t, :], idf_sb[:, t : t + 1], inv_abs[c][:, t, :], ALU.mult, ALU.mult
                 )
 
         def make_z(c):
@@ -197,22 +194,21 @@ def tile_picked_none_p_kernel(tc, x_words, x_scales, w1, lengths, idf, w2, offs,
             z_codes = keep.tile([P, CHUNK], U32, name=f"z_codes{c}", align_bytes=64)
             z_scale = keep.tile([P, CHUNK], U8, name=f"z_scale{c}", align_bytes=64)
             nc.vector.quantize_mx(z_codes[:].bitcast(FP8X4), z_scale[:], z_bf[c][:].rearrange("p n t -> p (n t)"))
-            row_blocks = N // P
             if c < CHUNKS - 1:
-                bank = second_product(z_codes, z_scale, range(row_blocks), f"second{c}")
-                result = keep.tile([P, row_blocks, CHUNK], F32, name=f"result{c}", align_bytes=64)
+                bank = second_product(z_codes, z_scale, range(ROW_BLOCKS), f"second{c}")
+                result = keep.tile([P, ROW_BLOCKS, CHUNK], F32, name=f"result{c}", align_bytes=64)
                 nc.scalar.copy(result[:], bank[:])
                 nc.sync.dma_start(out_rows[:, :, places], result[:])
             else:
-                split = row_blocks // 2
-                bank = second_product(z_codes, z_scale, range(split), f"second{c}")
-                upper = keep.tile([P, split, CHUNK], F32, name="upper", align_bytes=64)
-                nc.scalar.copy(upper[:], bank[:])
-                nc.scalar.dma_start(out_rows[:, :split, places], upper[:])
-                bank = second_product(z_codes, z_scale, range(split, row_blocks), "first0")
-                lower = keep.tile([P, split, CHUNK], F32, name="lower", align_bytes=64)
-                nc.vector.tensor_copy(lower[:], bank[:])
-                nc.sync.dma_start(out_rows[:, split:, places], lower[:])
+                for b, tag in enumerate((f"second{c}", "first0", "first1", "first2")):
+                    bank = second_product(z_codes, z_scale, range(b, b + 1), tag)
+                    result = keep.tile([P, 1, CHUNK], F32, name=f"last{b}", align_bytes=64)
+                    if b % 2 == 0:
+                        nc.scalar.copy(result[:], bank[:])
+                        nc.scalar.dma_start(out_rows[:, b : b + 1, places], result[:])
+                    else:
+                        nc.vector.tensor_copy(result[:], bank[:])
+                        nc.sync.dma_start(out_rows[:, b : b + 1, places], result[:])
 
         make_denominator(0)
         make_denominator(1)

@@ -45,6 +45,9 @@ def tile_picked_none_p_kernel(tc, x_words, x_scales, w1, lengths, idf, w2, offs,
         offs_sb = keep.tile([P, S // PER_COL], U16, name="offs_sb")
         doc_sb = keep.tile([P, S // PER_COL], U16, name="doc_sb")
 
+        idf_sb = keep.tile([P, PACK], F32, name="idf_sb")
+        nc.scalar.dma_start(idf_sb[:], idf.rearrange("(p t) o -> p (t o)", t=PACK))
+
         warm = keep.tile([P, 2], F32, name="warm")
         nc.vector.memset(warm[:, 0:1], 1.0)
         nc.scalar.activation(warm[:, 1:2], warm[:, 0:1], ACT.Abs_reciprocal_sqrt)
@@ -53,6 +56,9 @@ def tile_picked_none_p_kernel(tc, x_words, x_scales, w1, lengths, idf, w2, offs,
         nc.vector.memset(scale_table[:].bitcast(I32), 0)
         x_scale = keep.tile([P, S], U8, name="x_scale", align_bytes=64)
         nc.gpsimd.memset(x_scale[:].bitcast(I32), 0)
+
+        inv_idf = keep.tile([P, PACK], F32, name="inv_idf")
+        nc.vector.reciprocal(inv_idf[:], idf_sb[:])
 
         len_rows = lengths.rearrange("(p t) u -> p t u", t=PACK)
         w2_half_bytes = PACK * W2_HALF * F32_BYTES
@@ -93,8 +99,6 @@ def tile_picked_none_p_kernel(tc, x_words, x_scales, w1, lengths, idf, w2, offs,
             raw = shared.tile([P, PACK, W2_HALF], F32, name=f"w2_raw{h}", align_bytes=64, offset=h * w2_half_bytes)
             nc.sync.dma_start(raw[:], w2_rows[:, :, h * W2_HALF : (h + 1) * W2_HALF])
             w2_raw.append(raw)
-        idf_sb = keep.tile([P, PACK], F32, name="idf_sb")
-        nc.sync.dma_start(idf_sb[:], idf.rearrange("(p t) o -> p (t o)", t=PACK))
 
         w1_codes = keep.tile([P, H], U32, name="w1_codes", align_bytes=64)
         w1_scale = keep.tile([P, H], U8, name="w1_scale", align_bytes=64)
@@ -118,60 +122,77 @@ def tile_picked_none_p_kernel(tc, x_words, x_scales, w1, lengths, idf, w2, offs,
         w2_codes = keep.tile([P, N], U32, name="w2_codes", align_bytes=64)
         w2_scale = keep.tile([P, N], U8, name="w2_scale", align_bytes=64)
 
-        first = []
-        for c in range(CHUNKS):
-            h, start = divmod(c * CHUNK, HALF)
-            bank = psum.tile([P, PACK, CHUNK], F32, name=f"first{c}", tag=f"first{c}")
-            for t in range(PACK):
-                feats = slice(t * P, (t + 1) * P)
-                nc.tensor.matmul_mx(
-                    bank[:, t, :],
-                    lhsT=w1_codes[:, feats].bitcast(FP8X4),
-                    lhsT_scale=w1_scale[:, feats],
-                    rhs=x_codes[h][:, start : start + CHUNK].bitcast(FP8X4),
-                    rhs_scale=x_scale[:, c * CHUNK : (c + 1) * CHUNK],
-                    start=True,
-                    stop=True,
-                )
-            first.append(bank)
+        first = {}
+        for h in range(2):
+            for pair in range(2):
+                bank = psum.tile([P, 2, HALF], F32, name=f"first{h}{pair}", tag=f"first{h}{pair}")
+                for e in range(2):
+                    feats = slice((2 * pair + e) * P, (2 * pair + e + 1) * P)
+                    nc.tensor.matmul_mx(
+                        bank[:, e, :],
+                        lhsT=w1_codes[:, feats].bitcast(FP8X4),
+                        lhsT_scale=w1_scale[:, feats],
+                        rhs=x_codes[h][:].bitcast(FP8X4),
+                        rhs_scale=x_scale[:, h * HALF : (h + 1) * HALF],
+                        start=True,
+                        stop=True,
+                    )
+                first[h, pair] = bank
 
         out_rows = out.rearrange("(b p) s -> p b s", p=P)
 
-        def per_chunk(name):
-            return [keep.tile([P, PACK, CHUNK], F32, name=f"{name}{c}", align_bytes=64) for c in range(CHUNKS)]
+        def per_half(name):
+            return [keep.tile([P, PACK, HALF], F32, name=f"{name}{h}", align_bytes=64) for h in range(2)]
 
-        den, root, inv_abs, sign, factor = (per_chunk(name) for name in ("den", "root", "inv_abs", "sign", "factor"))
-        z_bf = [keep.tile([P, CHUNK, PACK], BF16, name=f"z_bf{c}", align_bytes=64) for c in range(CHUNKS)]
+        def pair_tile(name, h, pair, tag=None):
+            return keep.tile([P, 2, HALF], F32, name=f"{name}{h}{pair}", tag=tag or f"{name}{h}{pair}", align_bytes=64)
+
+        sign, size = per_half("sign"), per_half("size")
+        den, root, inv_abs = {}, {}, {}
+        z_bf = [keep.tile([P, CHUNK, PACK], BF16, name=f"z_bf{c}", tag=f"z_bf{c}", align_bytes=64) for c in range(CHUNKS)]
+
+        def in_half(tiles, c):
+            h, start = divmod(c * CHUNK, HALF)
+            return tiles[h][:, :, start : start + CHUNK]
 
         def quantise_w2(h):
             cols = slice(h * W2_HALF, (h + 1) * W2_HALF)
             nc.vector.quantize_mx(w2_codes[:, cols].bitcast(FP8X4), w2_scale[:, cols], w2_bf[:, cols, :].rearrange("p c j -> p (c j)"))
 
-        def make_denominator(c):
-            nc.vector.scalar_tensor_tensor(den[c][:], first[c][:], 0.0, len_picked[:, :, c * CHUNK : (c + 1) * CHUNK], ALU.max, ALU.add)
+        def make_denominator(h, pair):
+            den[h, pair] = pair_tile("den", h, pair)
+            picked = len_picked[:, 2 * pair : 2 * pair + 2, h * HALF : (h + 1) * HALF]
+            nc.vector.scalar_tensor_tensor(den[h, pair][:], first[h, pair][:], 0.0, picked, ALU.max, ALU.add)
 
-        def make_root(c):
-            nc.scalar.activation(root[c][:], den[c][:], ACT.Abs_reciprocal_sqrt)
+        def make_root(h, t):
+            nc.scalar.activation(root[h, t // 2][:, t % 2, :], den[h, t // 2][:, t % 2, :], ACT.Abs_reciprocal_sqrt, scale=inv_idf[:, t : t + 1])
 
-        def make_inverse(c):
-            gain = 4.0 if c == VECTOR_SIGN_CHUNK else 2.0
-            nc.scalar.activation(inv_abs[c][:], root[c][:], ACT.Square, scale=math.sqrt(gain))
+        def make_sign(h, t, cols):
+            nc.scalar.activation(sign[h][:, t, cols], den[h, t // 2][:, t % 2, cols], ACT.Sign, scale=inv_idf[:, t : t + 1])
 
-        def make_sign(c):
-            if c == VECTOR_SIGN_CHUNK:
-                nc.vector.tensor_scalar(sign[c][:], den[c][:], 0.0, 0.5, ALU.is_ge, ALU.subtract)
-            else:
-                nc.scalar.activation(sign[c][:], den[c][:], ACT.Sign)
+        def make_inverse(h, pair, cols):
+            nc.scalar.activation(inv_abs[h, pair][:, :, cols], root[h, pair][:, :, cols], ACT.Square, scale=math.sqrt(2.0))
 
-        def make_factor(c):
-            for t in range(PACK):
-                nc.vector.scalar_tensor_tensor(
-                    factor[c][:, t, :], sign[c][:, t, :], idf_sb[:, t : t + 1], inv_abs[c][:, t, :], ALU.mult, ALU.mult
-                )
+        def make_pair_root(h, pair):
+            nc.scalar.activation(root[h, pair][:], den[h, pair][:], ACT.Abs_reciprocal_sqrt, scale=0.25)
+
+        def vector_sign(h, pair):
+            nc.vector.tensor_scalar(sign[h][:, 2 * pair : 2 * pair + 2, :], den[h, pair][:], 0.0, 0.5, ALU.is_ge, ALU.subtract)
+
+        def vector_inverse(h, t):
+            r = root[h, t // 2][:, t % 2, :]
+            nc.vector.scalar_tensor_tensor(inv_abs[h, t // 2][:, t % 2, :], r, idf_sb[:, t : t + 1], r, ALU.mult, ALU.mult)
+
+        def make_size(h, pair, cols):
+            planes = slice(2 * pair, 2 * pair + 2)
+            nc.vector.scalar_tensor_tensor(size[h][:, planes, cols], first[h, pair][:, :, cols], 0.0, inv_abs[h, pair][:, :, cols], ALU.max, ALU.mult)
 
         def make_z(c):
-            nc.vector.scalar_tensor_tensor(
-                z_bf[c][:], first[c][:].rearrange("p t n -> p n t"), 0.0, factor[c][:].rearrange("p t n -> p n t"), ALU.max, ALU.mult
+            nc.vector.tensor_tensor(
+                z_bf[c][:].rearrange("p (g i) t -> p g t i", i=LINE),
+                in_half(size, c).rearrange("p t (g i) -> p g t i", i=LINE),
+                in_half(sign, c).rearrange("p t (g i) -> p g t i", i=LINE),
+                ALU.mult,
             )
 
         def second_product(z_codes, z_scale, blocks, bank_tag):
@@ -196,11 +217,11 @@ def tile_picked_none_p_kernel(tc, x_words, x_scales, w1, lengths, idf, w2, offs,
             nc.vector.quantize_mx(z_codes[:].bitcast(FP8X4), z_scale[:], z_bf[c][:].rearrange("p n t -> p (n t)"))
             if c < CHUNKS - 1:
                 bank = second_product(z_codes, z_scale, range(ROW_BLOCKS), f"second{c}")
-                result = keep.tile([P, ROW_BLOCKS, CHUNK], F32, name=f"result{c}", align_bytes=64)
+                result = keep.tile([P, ROW_BLOCKS, CHUNK], F32, name=f"result{c}", tag=("den10", "den11", "result2")[c], align_bytes=64)
                 nc.scalar.copy(result[:], bank[:])
                 nc.sync.dma_start(out_rows[:, :, places], result[:])
             else:
-                for b, tag in enumerate((f"second{c}", "first0", "first1", "first2")):
+                for b, tag in enumerate((f"second{c}", "first00", "first01", "first10")):
                     bank = second_product(z_codes, z_scale, range(b, b + 1), tag)
                     result = keep.tile([P, 1, CHUNK], F32, name=f"last{b}", align_bytes=64)
                     if b % 2 == 0:
@@ -210,27 +231,40 @@ def tile_picked_none_p_kernel(tc, x_words, x_scales, w1, lengths, idf, w2, offs,
                         nc.vector.tensor_copy(result[:], bank[:])
                         nc.sync.dma_start(out_rows[:, b : b + 1, places], result[:])
 
-        make_denominator(0)
-        make_denominator(1)
-        make_root(0)
-        make_root(1)
-        make_inverse(0)
-        make_sign(1)
-        make_inverse(1)
-        make_denominator(2)
-        make_denominator(3)
-        make_sign(0)
-        for c in range(2, CHUNKS):
-            make_root(c)
-            make_sign(c)
-            make_inverse(c)
+        whole, low, high = slice(0, HALF), slice(0, CHUNK), slice(CHUNK, HALF)
+        for h in range(2):
+            for pair in range(2):
+                make_denominator(h, pair)
+                root[h, pair] = pair_tile("root", h, pair)
+                inv_abs[h, pair] = pair_tile("inv_abs", h, pair)
+        for t in range(PACK):
+            make_root(0, t)
+        make_inverse(0, 0, whole)
+        make_sign(0, 0, whole)
+        make_inverse(0, 1, whole)
+        for t in range(1, PACK):
+            make_sign(0, t, whole)
+        for t in range(PACK):
+            make_root(1, t)
+        make_inverse(1, 0, whole)
+        make_sign(1, 0, whole)
+        make_inverse(1, 1, whole)
+        for cols in (low, high):
+            for t in range(1, PACK):
+                make_sign(1, t, cols)
 
         quantise_w2(0)
-        make_factor(0)
+        make_size(0, 0, whole)
         quantise_w2(1)
+        make_size(0, 1, whole)
         make_z(0)
-        for c in range(1, CHUNKS):
-            make_factor(c)
-            project(c - 1)
-            make_z(c)
-        project(CHUNKS - 1)
+        make_z(1)
+        project(0)
+        make_size(1, 0, whole)
+        project(1)
+        make_size(1, 1, low)
+        make_z(2)
+        make_size(1, 1, high)
+        project(2)
+        make_z(3)
+        project(3)

@@ -170,14 +170,14 @@ def tile_picked_none_p_kernel(tc, x_words, x_scales, w1, lengths, idf, w2, offs,
         def make_sign(h, t, cols):
             nc.scalar.activation(sign[h][:, t, cols], den[h, t // 2][:, t % 2, cols], ACT.Sign, scale=inv_idf[:, t : t + 1])
 
-        def make_inverse(h, pair, cols):
-            nc.scalar.activation(inv_abs[h, pair][:, :, cols], root[h, pair][:, :, cols], ACT.Square, scale=math.sqrt(2.0))
+        def make_inverse(h, pair, planes):
+            nc.scalar.activation(inv_abs[h, pair][:, planes, :], root[h, pair][:, planes, :], ACT.Square, scale=math.sqrt(2.0))
 
-        def make_pair_root(h, pair):
-            nc.scalar.activation(root[h, pair][:], den[h, pair][:], ACT.Abs_reciprocal_sqrt, scale=0.25)
+        def plain_root(h, t):
+            nc.scalar.activation(root[h, t // 2][:, t % 2, :], den[h, t // 2][:, t % 2, :], ACT.Abs_reciprocal_sqrt, scale=0.25)
 
-        def vector_sign(h, pair):
-            nc.vector.tensor_scalar(sign[h][:, 2 * pair : 2 * pair + 2, :], den[h, pair][:], 0.0, 0.5, ALU.is_ge, ALU.subtract)
+        def vector_sign(h, t):
+            nc.vector.tensor_scalar(sign[h][:, t, :], den[h, t // 2][:, t % 2, :], 0.0, 0.5, ALU.is_ge, ALU.subtract)
 
         def vector_inverse(h, t):
             r = root[h, t // 2][:, t % 2, :]
@@ -215,48 +215,54 @@ def tile_picked_none_p_kernel(tc, x_words, x_scales, w1, lengths, idf, w2, offs,
             z_codes = keep.tile([P, CHUNK], U32, name=f"z_codes{c}", align_bytes=64)
             z_scale = keep.tile([P, CHUNK], U8, name=f"z_scale{c}", align_bytes=64)
             nc.vector.quantize_mx(z_codes[:].bitcast(FP8X4), z_scale[:], z_bf[c][:].rearrange("p n t -> p (n t)"))
-            if c < CHUNKS - 1:
-                bank = second_product(z_codes, z_scale, range(ROW_BLOCKS), f"second{c}")
-                result = keep.tile([P, ROW_BLOCKS, CHUNK], F32, name=f"result{c}", tag=("den10", "den11", "result2")[c], align_bytes=64)
-                nc.scalar.copy(result[:], bank[:])
-                nc.sync.dma_start(out_rows[:, :, places], result[:])
-            else:
-                for b, tag in enumerate((f"second{c}", "first00", "first01", "first10")):
-                    bank = second_product(z_codes, z_scale, range(b, b + 1), tag)
-                    result = keep.tile([P, 1, CHUNK], F32, name=f"last{b}", align_bytes=64)
-                    if b % 2 == 0:
-                        nc.scalar.copy(result[:], bank[:])
-                        nc.scalar.dma_start(out_rows[:, b : b + 1, places], result[:])
-                    else:
-                        nc.vector.tensor_copy(result[:], bank[:])
-                        nc.sync.dma_start(out_rows[:, b : b + 1, places], result[:])
+            for blocks, bank_tag, result_tag in exits[c]:
+                bank = second_product(z_codes, z_scale, blocks, bank_tag)
+                result = keep.tile([P, len(blocks), CHUNK], F32, name=f"result{c}{blocks.start}", tag=result_tag, align_bytes=64)
+                on_vector = c == CHUNKS - 1 and blocks.stop < ROW_BLOCKS
+                if on_vector:
+                    nc.vector.tensor_copy(result[:], bank[:])
+                else:
+                    nc.scalar.copy(result[:], bank[:])
+                (nc.sync if on_vector or c < CHUNKS - 2 else nc.scalar).dma_start(out_rows[:, blocks.start : blocks.stop, places], result[:])
 
+        exits = [
+            [(range(0, 4), "second0", "den10")],
+            [(range(0, 4), "second1", "den11")],
+            [(range(0, 2), "second2", "result20"), (range(2, 4), "first00", "result22")],
+            [(range(b, b + 1), tag, f"result3{b}") for b, tag in enumerate(("second3", "first01", "first10", "first11"))],
+        ]
         whole, low, high = slice(0, HALF), slice(0, CHUNK), slice(CHUNK, HALF)
+        both = slice(0, 2)
         for h in range(2):
             for pair in range(2):
                 make_denominator(h, pair)
                 root[h, pair] = pair_tile("root", h, pair)
                 inv_abs[h, pair] = pair_tile("inv_abs", h, pair)
-        for t in range(PACK):
-            make_root(0, t)
-        make_inverse(0, 0, whole)
-        make_sign(0, 0, whole)
-        make_inverse(0, 1, whole)
-        for t in range(1, PACK):
-            make_sign(0, t, whole)
+        make_root(0, 1)
+        plain_root(0, 0)
+        make_root(0, 2)
+        make_root(0, 3)
+        make_inverse(0, 0, slice(1, 2))
+        make_sign(0, 1, whole)
+        make_sign(0, 2, whole)
+        make_inverse(0, 1, both)
+        make_sign(0, 3, whole)
         for t in range(PACK):
             make_root(1, t)
-        make_inverse(1, 0, whole)
+        make_inverse(1, 0, both)
         make_sign(1, 0, whole)
-        make_inverse(1, 1, whole)
+        make_inverse(1, 1, both)
         for cols in (low, high):
             for t in range(1, PACK):
                 make_sign(1, t, cols)
 
         quantise_w2(0)
+        vector_inverse(0, 0)
+        vector_sign(0, 0)
         make_size(0, 0, whole)
         quantise_w2(1)
-        make_size(0, 1, whole)
+        make_size(0, 1, low)
+        make_size(0, 1, high)
         make_z(0)
         make_z(1)
         project(0)

@@ -119,8 +119,7 @@ def tile_picked_none_p_kernel(tc, x_words, x_scales, w1, lengths, idf, w2, offs,
             h, start = divmod(col, W2_HALF)
             piece = w2_raw[h][:, :, start : start + W2_PIECE].rearrange("p j c -> p c j")
             nc.gpsimd.tensor_scalar(w2_bf[:, col : col + W2_PIECE, :], piece, 1.0, 0.0, ALU.mult, ALU.add)
-        w2_codes = keep.tile([P, N], U32, name="w2_codes", align_bytes=64)
-        w2_scale = keep.tile([P, N], U8, name="w2_scale", align_bytes=64)
+        w2_codes, w2_scale = [], []
 
         first = {}
         for h in range(2):
@@ -155,9 +154,17 @@ def tile_picked_none_p_kernel(tc, x_words, x_scales, w1, lengths, idf, w2, offs,
             h, start = divmod(c * CHUNK, HALF)
             return tiles[h][:, :, start : start + CHUNK]
 
-        def quantise_w2(h):
+        def quantise_w2(h, tag):
             cols = slice(h * W2_HALF, (h + 1) * W2_HALF)
-            nc.vector.quantize_mx(w2_codes[:, cols].bitcast(FP8X4), w2_scale[:, cols], w2_bf[:, cols, :].rearrange("p c j -> p (c j)"))
+            w2_codes.append(keep.tile([P, W2_HALF], U32, name=f"w2_codes{h}", tag=tag, align_bytes=64))
+            w2_scale.append(keep.tile([P, W2_HALF], U8, name=f"w2_scale{h}", align_bytes=64))
+            nc.vector.quantize_mx(w2_codes[h][:].bitcast(FP8X4), w2_scale[h][:], w2_bf[:, cols, :].rearrange("p c j -> p (c j)"))
+
+        def warm_up(codes, scale, bank_tag):
+            bank = psum.tile([P, H], F32, name=f"warm_{bank_tag}", tag=bank_tag)
+            nc.tensor.matmul_mx(
+                bank[:], lhsT=codes.bitcast(FP8X4), lhsT_scale=scale, rhs=w1_codes[:].bitcast(FP8X4), rhs_scale=w1_scale[:], start=True, stop=True
+            )
 
         def make_denominator(h, pair):
             den[h, pair] = pair_tile("den", h, pair)
@@ -198,11 +205,11 @@ def tile_picked_none_p_kernel(tc, x_words, x_scales, w1, lengths, idf, w2, offs,
         def second_product(z_codes, z_scale, blocks, bank_tag):
             bank = psum.tile([P, blocks.stop - blocks.start, CHUNK], F32, name=bank_tag, tag=bank_tag)
             for b in blocks:
-                rows = slice(b * P, (b + 1) * P)
+                rows = slice(b % 2 * P, (b % 2 + 1) * P)
                 nc.tensor.matmul_mx(
                     bank[:, b - blocks.start, :],
-                    lhsT=w2_codes[:, rows].bitcast(FP8X4),
-                    lhsT_scale=w2_scale[:, rows],
+                    lhsT=w2_codes[b // 2][:, rows].bitcast(FP8X4),
+                    lhsT_scale=w2_scale[b // 2][:, rows],
                     rhs=z_codes[:].bitcast(FP8X4),
                     rhs_scale=z_scale[:],
                     start=True,
@@ -224,12 +231,13 @@ def tile_picked_none_p_kernel(tc, x_words, x_scales, w1, lengths, idf, w2, offs,
                 else:
                     nc.scalar.copy(result[:], bank[:])
                 (nc.sync if on_vector or c < CHUNKS - 2 else nc.scalar).dma_start(out_rows[:, blocks.start : blocks.stop, places], result[:])
+            return z_codes, z_scale
 
         exits = [
             [(range(0, 4), "second0", "den10")],
             [(range(0, 4), "second1", "den11")],
             [(range(0, 2), "second2", "result20"), (range(2, 4), "first00", "result22")],
-            [(range(b, b + 1), tag, f"result3{b}") for b, tag in enumerate(("second3", "first01", "first10", "first11"))],
+            [(range(b, b + 1), tag, f"result3{b}") for b, tag in enumerate(("second3", "second0", "first10", "first11"))],
         ]
         whole, low, high = slice(0, HALF), slice(0, CHUNK), slice(CHUNK, HALF)
         both = slice(0, 2)
@@ -256,18 +264,20 @@ def tile_picked_none_p_kernel(tc, x_words, x_scales, w1, lengths, idf, w2, offs,
             for t in range(1, PACK):
                 make_sign(1, t, cols)
 
-        quantise_w2(0)
+        quantise_w2(0, "w2_codes0")
         vector_inverse(0, 0)
         vector_sign(0, 0)
         make_size(0, 0, whole)
-        quantise_w2(1)
         make_size(0, 1, low)
-        make_size(0, 1, high)
+        quantise_w2(1, "w2_codes1")
         make_z(0)
-        make_z(1)
+        make_size(0, 1, high)
+        warm_up(w2_codes[0][:, :P], w2_scale[0][:, :P], "first01")
         project(0)
+        make_z(1)
         make_size(1, 0, whole)
-        project(1)
+        codes, scale = project(1)
+        warm_up(codes[:], scale[:], "second3")
         make_size(1, 1, low)
         make_z(2)
         make_size(1, 1, high)

@@ -27,7 +27,6 @@ ROW_BLOCKS = N // P
 HALF = S // 2
 W2_HALF = N // 2
 W2_PIECE = N // 4
-VECTOR_SIGN_CHUNK = 0
 F32_BYTES = 4
 LINE = 4
 
@@ -57,8 +56,10 @@ def tile_picked_none_p_kernel(tc, x_words, x_scales, w1, lengths, idf, w2, offs,
         x_scale = keep.tile([P, S], U8, name="x_scale", align_bytes=64)
         nc.gpsimd.memset(x_scale[:].bitcast(I32), 0)
 
-        inv_idf = keep.tile([P, PACK], F32, name="inv_idf")
-        nc.vector.reciprocal(inv_idf[:], idf_sb[:])
+        idf_sign = keep.tile([P, PACK], F32, name="idf_sign")
+        nc.scalar.activation(idf_sign[:], idf_sb[:], ACT.Sign)
+        idf_or_one = keep.tile([P, PACK], F32, name="idf_or_one")
+        nc.vector.scalar_tensor_tensor(idf_or_one[:], idf_sb[:], 0.0, idf_sb[:], ALU.is_equal, ALU.add)
 
         len_rows = lengths.rearrange("(p t) u -> p t u", t=PACK)
         w2_half_bytes = PACK * W2_HALF * F32_BYTES
@@ -85,6 +86,9 @@ def tile_picked_none_p_kernel(tc, x_words, x_scales, w1, lengths, idf, w2, offs,
         for t in range(PACK):
             for h in range(2):
                 nc.vector.tensor_copy(len_picked[:, t, h * HALF : (h + 1) * HALF], len_sb[t][:].indirect(half_of_list(doc_sb, h)))
+
+        inv_idf = keep.tile([P, PACK], F32, name="inv_idf")
+        nc.vector.reciprocal(inv_idf[:], idf_or_one[:])
 
         w1_bf = keep.tile([P, PACK, P, PACK], BF16, name="w1_bf", tag="w1_bf", align_bytes=64)
         for h in range(2):
@@ -119,7 +123,6 @@ def tile_picked_none_p_kernel(tc, x_words, x_scales, w1, lengths, idf, w2, offs,
             h, start = divmod(col, W2_HALF)
             piece = w2_raw[h][:, :, start : start + W2_PIECE].rearrange("p j c -> p c j")
             nc.gpsimd.tensor_scalar(w2_bf[:, col : col + W2_PIECE, :], piece, 1.0, 0.0, ALU.mult, ALU.add)
-        w2_codes, w2_scale = [], []
 
         first = {}
         for h in range(2):
@@ -139,83 +142,75 @@ def tile_picked_none_p_kernel(tc, x_words, x_scales, w1, lengths, idf, w2, offs,
                 first[h, pair] = bank
 
         out_rows = out.rearrange("(b p) s -> p b s", p=P)
+        all_places, low, high = slice(0, HALF), slice(0, CHUNK), slice(CHUNK, HALF)
+        both_planes = slice(0, 2)
 
         def per_half(name):
             return [keep.tile([P, PACK, HALF], F32, name=f"{name}{h}", align_bytes=64) for h in range(2)]
 
-        def pair_tile(name, h, pair, tag=None):
-            return keep.tile([P, 2, HALF], F32, name=f"{name}{h}{pair}", tag=tag or f"{name}{h}{pair}", align_bytes=64)
+        def pair_tile(name, h, pair):
+            return keep.tile([P, 2, HALF], F32, name=f"{name}{h}{pair}", tag=f"{name}{h}{pair}", align_bytes=64)
+
+        def plane_of(tiles, h, t):
+            return tiles[h, t // 2][:, t % 2, :]
+
+        def chunk_by_lines(tiles, c):
+            h, start = divmod(c * CHUNK, HALF)
+            return tiles[h][:, :, start : start + CHUNK].rearrange("p t (g i) -> p g t i", i=LINE)
 
         sign, size = per_half("sign"), per_half("size")
-        den, root, inv_abs = {}, {}, {}
-        z_bf = [keep.tile([P, CHUNK, PACK], BF16, name=f"z_bf{c}", tag=f"z_bf{c}", align_bytes=64) for c in range(CHUNKS)]
+        den, root, weight = {}, {}, {}
+        z_bf = [keep.tile([P, CHUNK, PACK], BF16, name=f"z_bf{c}", align_bytes=64) for c in range(CHUNKS)]
+        w2_codes, w2_scale = [], []
 
-        def in_half(tiles, c):
-            h, start = divmod(c * CHUNK, HALF)
-            return tiles[h][:, :, start : start + CHUNK]
-
-        def quantise_w2(h, tag):
+        def quantise_w2(h):
             cols = slice(h * W2_HALF, (h + 1) * W2_HALF)
-            w2_codes.append(keep.tile([P, W2_HALF], U32, name=f"w2_codes{h}", tag=tag, align_bytes=64))
+            w2_codes.append(keep.tile([P, W2_HALF], U32, name=f"w2_codes{h}", align_bytes=64))
             w2_scale.append(keep.tile([P, W2_HALF], U8, name=f"w2_scale{h}", align_bytes=64))
             nc.vector.quantize_mx(w2_codes[h][:].bitcast(FP8X4), w2_scale[h][:], w2_bf[:, cols, :].rearrange("p c j -> p (c j)"))
 
-        def warm_up(codes, scale, bank_tag):
-            bank = psum.tile([P, H], F32, name=f"warm_{bank_tag}", tag=bank_tag)
-            nc.tensor.matmul_mx(
-                bank[:], lhsT=codes.bitcast(FP8X4), lhsT_scale=scale, rhs=w1_codes[:].bitcast(FP8X4), rhs_scale=w1_scale[:], start=True, stop=True
-            )
-
         def make_denominator(h, pair):
-            den[h, pair] = pair_tile("den", h, pair)
             picked = len_picked[:, 2 * pair : 2 * pair + 2, h * HALF : (h + 1) * HALF]
             nc.vector.scalar_tensor_tensor(den[h, pair][:], first[h, pair][:], 0.0, picked, ALU.max, ALU.add)
 
         def make_root(h, t):
-            nc.scalar.activation(root[h, t // 2][:, t % 2, :], den[h, t // 2][:, t % 2, :], ACT.Abs_reciprocal_sqrt, scale=inv_idf[:, t : t + 1])
+            nc.scalar.activation(plane_of(root, h, t), plane_of(den, h, t), ACT.Abs_reciprocal_sqrt, scale=inv_idf[:, t : t + 1])
+
+        def make_weight(h, pair, planes):
+            nc.scalar.activation(weight[h, pair][:, planes, :], root[h, pair][:, planes, :], ACT.Square, scale=math.sqrt(2.0))
 
         def make_sign(h, t, cols):
-            nc.scalar.activation(sign[h][:, t, cols], den[h, t // 2][:, t % 2, cols], ACT.Sign, scale=inv_idf[:, t : t + 1])
-
-        def make_inverse(h, pair, planes):
-            nc.scalar.activation(inv_abs[h, pair][:, planes, :], root[h, pair][:, planes, :], ACT.Square, scale=math.sqrt(2.0))
-
-        def plain_root(h, t):
-            nc.scalar.activation(root[h, t // 2][:, t % 2, :], den[h, t // 2][:, t % 2, :], ACT.Abs_reciprocal_sqrt, scale=0.25)
-
-        def vector_sign(h, t):
-            nc.vector.tensor_scalar(sign[h][:, t, :], den[h, t // 2][:, t % 2, :], 0.0, 0.5, ALU.is_ge, ALU.subtract)
-
-        def vector_inverse(h, t):
-            r = root[h, t // 2][:, t % 2, :]
-            nc.vector.scalar_tensor_tensor(inv_abs[h, t // 2][:, t % 2, :], r, idf_sb[:, t : t + 1], r, ALU.mult, ALU.mult)
+            nc.scalar.activation(sign[h][:, t, cols], plane_of(den, h, t)[:, cols], ACT.Sign, scale=idf_sign[:, t : t + 1])
 
         def make_size(h, pair, cols):
             planes = slice(2 * pair, 2 * pair + 2)
-            nc.vector.scalar_tensor_tensor(size[h][:, planes, cols], first[h, pair][:, :, cols], 0.0, inv_abs[h, pair][:, :, cols], ALU.max, ALU.mult)
+            nc.vector.scalar_tensor_tensor(size[h][:, planes, cols], first[h, pair][:, :, cols], 0.0, weight[h, pair][:, :, cols], ALU.max, ALU.mult)
 
         def make_z(c):
-            nc.vector.tensor_tensor(
-                z_bf[c][:].rearrange("p (g i) t -> p g t i", i=LINE),
-                in_half(size, c).rearrange("p t (g i) -> p g t i", i=LINE),
-                in_half(sign, c).rearrange("p t (g i) -> p g t i", i=LINE),
-                ALU.mult,
-            )
+            woven = z_bf[c][:].rearrange("p (g i) t -> p g t i", i=LINE)
+            nc.vector.tensor_tensor(woven, chunk_by_lines(size, c), chunk_by_lines(sign, c), ALU.mult)
 
         def second_product(z_codes, z_scale, blocks, bank_tag):
-            bank = psum.tile([P, blocks.stop - blocks.start, CHUNK], F32, name=bank_tag, tag=bank_tag)
+            bank = psum.tile([P, len(blocks), CHUNK], F32, name=bank_tag, tag=bank_tag)
             for b in blocks:
-                rows = slice(b % 2 * P, (b % 2 + 1) * P)
+                h, start = divmod(b * P, W2_HALF)
                 nc.tensor.matmul_mx(
                     bank[:, b - blocks.start, :],
-                    lhsT=w2_codes[b // 2][:, rows].bitcast(FP8X4),
-                    lhsT_scale=w2_scale[b // 2][:, rows],
+                    lhsT=w2_codes[h][:, start : start + P].bitcast(FP8X4),
+                    lhsT_scale=w2_scale[h][:, start : start + P],
                     rhs=z_codes[:].bitcast(FP8X4),
                     rhs_scale=z_scale[:],
                     start=True,
                     stop=True,
                 )
             return bank
+
+        exits = [
+            [(range(0, 4), "second0", "den10")],
+            [(range(0, 4), "second1", "den11")],
+            [(range(0, 2), "second2", "result20"), (range(2, 4), "first00", "result22")],
+            [(range(b, b + 1), tag, f"result3{b}") for b, tag in enumerate(("second3", "second0", "first10", "first11"))],
+        ]
 
         def project(c):
             places = slice(c * CHUNK, (c + 1) * CHUNK)
@@ -230,54 +225,58 @@ def tile_picked_none_p_kernel(tc, x_words, x_scales, w1, lengths, idf, w2, offs,
                     nc.vector.tensor_copy(result[:], bank[:])
                 else:
                     nc.scalar.copy(result[:], bank[:])
-                (nc.sync if on_vector or c < CHUNKS - 2 else nc.scalar).dma_start(out_rows[:, blocks.start : blocks.stop, places], result[:])
+                queue = nc.sync if on_vector or c < CHUNKS // 2 else nc.scalar
+                queue.dma_start(out_rows[:, blocks.start : blocks.stop, places], result[:])
             return z_codes, z_scale
 
-        exits = [
-            [(range(0, 4), "second0", "den10")],
-            [(range(0, 4), "second1", "den11")],
-            [(range(0, 2), "second2", "result20"), (range(2, 4), "first00", "result22")],
-            [(range(b, b + 1), tag, f"result3{b}") for b, tag in enumerate(("second3", "second0", "first10", "first11"))],
-        ]
-        whole, low, high = slice(0, HALF), slice(0, CHUNK), slice(CHUNK, HALF)
-        both = slice(0, 2)
+        def warm_up(codes, scale, bank_tag):
+            bank = psum.tile([P, H], F32, name=f"warm_{bank_tag}", tag=bank_tag)
+            nc.tensor.matmul_mx(
+                bank[:], lhsT=codes.bitcast(FP8X4), lhsT_scale=scale, rhs=w1_codes[:].bitcast(FP8X4), rhs_scale=w1_scale[:], start=True, stop=True
+            )
+
         for h in range(2):
             for pair in range(2):
+                den[h, pair] = pair_tile("den", h, pair)
                 make_denominator(h, pair)
                 root[h, pair] = pair_tile("root", h, pair)
-                inv_abs[h, pair] = pair_tile("inv_abs", h, pair)
+                weight[h, pair] = pair_tile("weight", h, pair)
+
         make_root(0, 1)
-        plain_root(0, 0)
+        nc.scalar.activation(plane_of(root, 0, 0), plane_of(den, 0, 0), ACT.Abs_reciprocal_sqrt, scale=0.25)
         make_root(0, 2)
         make_root(0, 3)
-        make_inverse(0, 0, slice(1, 2))
-        make_sign(0, 1, whole)
-        make_sign(0, 2, whole)
-        make_inverse(0, 1, both)
-        make_sign(0, 3, whole)
+        make_weight(0, 0, slice(1, 2))
+        make_sign(0, 1, all_places)
+        make_sign(0, 2, all_places)
+        make_weight(0, 1, both_planes)
+        make_sign(0, 3, all_places)
+
         for t in range(PACK):
             make_root(1, t)
-        make_inverse(1, 0, both)
-        make_sign(1, 0, whole)
-        make_inverse(1, 1, both)
+        make_weight(1, 0, both_planes)
+        make_sign(1, 0, all_places)
+        make_weight(1, 1, both_planes)
         for cols in (low, high):
             for t in range(1, PACK):
                 make_sign(1, t, cols)
 
-        quantise_w2(0, "w2_codes0")
-        vector_inverse(0, 0)
-        vector_sign(0, 0)
-        make_size(0, 0, whole)
+        quantise_w2(0)
+        root_0 = plane_of(root, 0, 0)
+        nc.vector.scalar_tensor_tensor(plane_of(weight, 0, 0), root_0, idf_sb[:, 0:1], root_0, ALU.mult, ALU.mult)
+        nc.vector.tensor_scalar(sign[0][:, 0, :], plane_of(den, 0, 0), 0.0, 0.5, ALU.is_ge, ALU.subtract)
+
+        make_size(0, 0, all_places)
         make_size(0, 1, low)
-        quantise_w2(1, "w2_codes1")
+        quantise_w2(1)
         make_z(0)
         make_size(0, 1, high)
         warm_up(w2_codes[0][:, :P], w2_scale[0][:, :P], "first01")
         project(0)
         make_z(1)
-        make_size(1, 0, whole)
-        codes, scale = project(1)
-        warm_up(codes[:], scale[:], "second3")
+        make_size(1, 0, all_places)
+        chunk_1_codes, chunk_1_scale = project(1)
+        warm_up(chunk_1_codes[:], chunk_1_scale[:], "second3")
         make_size(1, 1, low)
         make_z(2)
         make_size(1, 1, high)

@@ -58,8 +58,6 @@ def tile_picked_none_p_kernel(tc, x_words, x_scales, w1, lengths, idf, w2, offs,
 
         idf_sign = keep.tile([P, PACK], F32, name="idf_sign")
         nc.scalar.activation(idf_sign[:], idf_sb[:], ACT.Sign)
-        idf_or_one = keep.tile([P, PACK], F32, name="idf_or_one")
-        nc.vector.scalar_tensor_tensor(idf_or_one[:], idf_sb[:], 0.0, idf_sb[:], ALU.is_equal, ALU.add)
 
         len_rows = lengths.rearrange("(p t) u -> p t u", t=PACK)
         w2_half_bytes = PACK * W2_HALF * F32_BYTES
@@ -70,11 +68,12 @@ def tile_picked_none_p_kernel(tc, x_words, x_scales, w1, lengths, idf, w2, offs,
         nc.sync.dma_start(offs_sb[:], offs)
         nc.sync.dma_start(scale_table[0:P:BLOCK_PARTS, :].bitcast(I32), x_scales[0].bitcast(I32))
         nc.sync.dma_start(len_sb[1][:], len_rows[:, 1, :])
-        w1_raw = keep.tile([P, PACK, H], F32, name="w1_raw", align_bytes=64)
+        w1_raw = keep.tile([P, PACK, H], F32, name="w1_raw", tag="w1_raw", align_bytes=64)
         nc.sync.dma_start(w1_raw[:], w1.rearrange("(p j) c -> p j c", j=PACK))
         for t in range(PACK // 2, PACK):
             nc.sync.dma_start(len_sb[t][:], len_rows[:, t, :])
-        word_table = keep.tile([P, T], U32, name="word_table", tag="word_table", align_bytes=64)
+        words_at = 2 * w2_half_bytes
+        word_table = shared.tile([P, T], U32, name="word_table", align_bytes=64, offset=words_at)
         nc.sync.dma_start(word_table[:].bitcast(I32), x_words[0].rearrange("p n r -> p (n r)").bitcast(I32))
 
         scale_picked = keep.tile([P, S], U8, name="scale_picked", align_bytes=64)
@@ -86,9 +85,6 @@ def tile_picked_none_p_kernel(tc, x_words, x_scales, w1, lengths, idf, w2, offs,
         for t in range(PACK):
             for h in range(2):
                 nc.vector.tensor_copy(len_picked[:, t, h * HALF : (h + 1) * HALF], len_sb[t][:].indirect(half_of_list(doc_sb, h)))
-
-        inv_idf = keep.tile([P, PACK], F32, name="inv_idf")
-        nc.vector.reciprocal(inv_idf[:], idf_or_one[:])
 
         w1_bf = keep.tile([P, PACK, P, PACK], BF16, name="w1_bf", tag="w1_bf", align_bytes=64)
         for h in range(2):
@@ -114,7 +110,12 @@ def tile_picked_none_p_kernel(tc, x_words, x_scales, w1, lengths, idf, w2, offs,
             nc.vector.tensor_copy(codes[:], word_table[:].indirect(half_of_list(offs_sb, h)))
             x_codes.append(codes)
 
-        w2_bf = keep.tile([P, N, PACK], BF16, name="w2_bf", tag="word_table", align_bytes=64)
+        idf_or_one = keep.tile([P, PACK], F32, name="idf_or_one", tag="w1_raw", align_bytes=64)
+        nc.vector.scalar_tensor_tensor(idf_or_one[:], idf_sb[:], 0.0, idf_sb[:], ALU.is_equal, ALU.add)
+        inv_idf = shared.tile([P, PACK], F32, name="inv_idf", align_bytes=64, offset=words_at + T * F32_BYTES // 2)
+        nc.vector.reciprocal(inv_idf[:], idf_or_one[:])
+
+        w2_bf = shared.tile([P, N, PACK], BF16, name="w2_bf", align_bytes=64, offset=words_at)
         nc.scalar.copy(
             w2_bf[:, :W2_PIECE, :].rearrange("p (c i) j -> p c j i", i=LINE),
             w2_raw[0][:, :, :W2_PIECE].rearrange("p j (c i) -> p c j i", i=LINE),

@@ -27,7 +27,7 @@ ROW_BLOCKS = N // P
 HALF = S // 2
 W2_HALF = N // 2
 W2_PIECE = N // 4
-F32_BYTES = 4
+PLANE_BYTES = U * 4
 LINE = 4
 
 
@@ -43,7 +43,6 @@ def tile_picked_none_p_kernel(tc, x_words, x_scales, w1, lengths, idf, w2, offs,
 
         offs_sb = keep.tile([P, S // PER_COL], U16, name="offs_sb")
         doc_sb = keep.tile([P, S // PER_COL], U16, name="doc_sb")
-
         idf_sb = keep.tile([P, PACK], F32, name="idf_sb")
         nc.scalar.dma_start(idf_sb[:], idf.rearrange("(p t) o -> p (t o)", t=PACK))
 
@@ -51,29 +50,24 @@ def tile_picked_none_p_kernel(tc, x_words, x_scales, w1, lengths, idf, w2, offs,
         nc.vector.memset(warm[:, 0:1], 1.0)
         nc.scalar.activation(warm[:, 1:2], warm[:, 0:1], ACT.Abs_reciprocal_sqrt)
 
-        scale_table = keep.tile([P, T], U8, name="scale_table", align_bytes=64)
+        w2_half_bytes = PACK * W2_HALF * 4
+        scale_table = shared.tile([P, T], U8, name="scale_table", align_bytes=64, offset=2 * w2_half_bytes)
         nc.vector.memset(scale_table[:].bitcast(I32), 0)
         x_scale = keep.tile([P, S], U8, name="x_scale", align_bytes=64)
         nc.gpsimd.memset(x_scale[:].bitcast(I32), 0)
 
-        idf_sign = keep.tile([P, PACK], F32, name="idf_sign")
-        nc.scalar.activation(idf_sign[:], idf_sb[:], ACT.Sign)
-
         len_rows = lengths.rearrange("(p t) u -> p t u", t=PACK)
-        w2_half_bytes = PACK * W2_HALF * F32_BYTES
-        len_sb = {t: keep.tile([P, U], F32, name=f"len_sb{t}", align_bytes=64) for t in range(PACK) if t != 1}
-        len_sb[1] = shared.tile([P, U], F32, name="len_sb1", align_bytes=64, offset=w2_half_bytes - U * F32_BYTES // 2)
+        len_sb = {t: keep.tile([P, U], F32, name=f"len_sb{t}", align_bytes=64) for t in (1, 2)}
+        len_sb[0] = shared.tile([P, U], F32, name="len_sb0", align_bytes=64, offset=w2_half_bytes - PLANE_BYTES // 2)
         nc.sync.dma_start(len_sb[0][:], len_rows[:, 0, :])
         nc.sync.dma_start(doc_sb[:], doc)
         nc.sync.dma_start(offs_sb[:], offs)
-        nc.sync.dma_start(scale_table[0:P:BLOCK_PARTS, :].bitcast(I32), x_scales[0].bitcast(I32))
         nc.sync.dma_start(len_sb[1][:], len_rows[:, 1, :])
-        w1_raw = keep.tile([P, PACK, H], F32, name="w1_raw", tag="w1_raw", align_bytes=64)
+        nc.sync.dma_start(scale_table[0:P:BLOCK_PARTS, :].bitcast(I32), x_scales[0].bitcast(I32))
+        w1_raw = keep.tile([P, PACK, H], F32, name="w1_raw", align_bytes=64)
         nc.sync.dma_start(w1_raw[:], w1.rearrange("(p j) c -> p j c", j=PACK))
-        for t in range(PACK // 2, PACK):
-            nc.sync.dma_start(len_sb[t][:], len_rows[:, t, :])
-        words_at = 2 * w2_half_bytes
-        word_table = shared.tile([P, T], U32, name="word_table", align_bytes=64, offset=words_at)
+        nc.sync.dma_start(len_sb[2][:], len_rows[:, 2, :])
+        word_table = keep.tile([P, T], U32, name="word_table", tag="word_table", align_bytes=64)
         nc.sync.dma_start(word_table[:].bitcast(I32), x_words[0].rearrange("p n r -> p (n r)").bitcast(I32))
 
         scale_picked = keep.tile([P, S], U8, name="scale_picked", align_bytes=64)
@@ -81,17 +75,28 @@ def tile_picked_none_p_kernel(tc, x_words, x_scales, w1, lengths, idf, w2, offs,
         for e in range(QUADRANT // BLOCK_PARTS):
             nc.scalar.dma_start(x_scale[e:P:QUADRANT, :].bitcast(I32), scale_picked[BLOCK_PARTS * e : P : QUADRANT, :].bitcast(I32))
 
-        len_picked = keep.tile([P, PACK, S], F32, name="len_picked", align_bytes=64)
-        for t in range(PACK):
-            for h in range(2):
-                nc.vector.tensor_copy(len_picked[:, t, h * HALF : (h + 1) * HALF], len_sb[t][:].indirect(half_of_list(doc_sb, h)))
+        len_sb[3] = shared.tile([P, U], F32, name="len_sb3", align_bytes=64, offset=2 * w2_half_bytes)
+        nc.sync.dma_start(len_sb[3][:], len_rows[:, 3, :])
 
-        w1_bf = keep.tile([P, PACK, P, PACK], BF16, name="w1_bf", tag="w1_bf", align_bytes=64)
-        for h in range(2):
-            nc.scalar.copy(
-                w1_bf[:, :, h * (P // 2) : (h + 1) * (P // 2), :].rearrange("p t m j -> p m j t"),
-                w1_raw[:, :, h * (H // 2) : (h + 1) * (H // 2)].rearrange("p j (m t) -> p m j t", t=PACK),
-            )
+        idf_sign = keep.tile([P, PACK], F32, name="idf_sign")
+        nc.scalar.activation(idf_sign[:], idf_sb[:], ACT.Sign)
+        idf_or_one = keep.tile([P, PACK], F32, name="idf_or_one")
+        nc.vector.scalar_tensor_tensor(idf_or_one[:], idf_sb[:], 0.0, idf_sb[:], ALU.is_equal, ALU.add)
+        inv_idf = keep.tile([P, PACK], F32, name="inv_idf")
+        nc.vector.reciprocal(inv_idf[:], idf_or_one[:])
+
+        def pair_tile(name, h, pair):
+            return keep.tile([P, 2, HALF], F32, name=f"{name}{h}{pair}", tag=f"{name}{h}{pair}", align_bytes=64)
+
+        def plane_of(tiles, h, t):
+            return tiles[h, t // 2][:, t % 2, :]
+
+        picked = {(h, pair): pair_tile("picked", h, pair) for h in range(2) for pair in range(2)}
+        for t, h in ((0, 0), (0, 1), (1, 0), (1, 1), (2, 0), (2, 1), (3, 0)):
+            nc.scalar.activation(plane_of(picked, h, t), len_sb[t][:].indirect(half_of_list(doc_sb, h)), ACT.Copy)
+
+        w1_bf = keep.tile([P, PACK, P, PACK], BF16, name="w1_bf", align_bytes=64)
+        nc.vector.tensor_copy(w1_bf[:].rearrange("p t m j -> p m j t"), w1_raw[:].rearrange("p j (m t) -> p m j t", t=PACK))
 
         w2_rows = w2.rearrange("(p j) c -> p j c", j=PACK)
         w2_raw = []
@@ -105,17 +110,13 @@ def tile_picked_none_p_kernel(tc, x_words, x_scales, w1, lengths, idf, w2, offs,
         nc.vector.quantize_mx(w1_codes[:].bitcast(FP8X4), w1_scale[:], w1_bf[:].rearrange("p t m j -> p (t m j)"))
 
         x_codes = []
-        for h, tag in enumerate(("x_codes", "w1_bf")):
-            codes = keep.tile([P, HALF], U32, name=f"x_codes{h}", tag=tag, align_bytes=64)
+        for h in range(2):
+            codes = keep.tile([P, HALF], U32, name=f"x_codes{h}", align_bytes=64)
             nc.vector.tensor_copy(codes[:], word_table[:].indirect(half_of_list(offs_sb, h)))
             x_codes.append(codes)
+        nc.vector.tensor_copy(plane_of(picked, 1, 3), len_sb[3][:].indirect(half_of_list(doc_sb, 1)))
 
-        idf_or_one = keep.tile([P, PACK], F32, name="idf_or_one", tag="w1_raw", align_bytes=64)
-        nc.vector.scalar_tensor_tensor(idf_or_one[:], idf_sb[:], 0.0, idf_sb[:], ALU.is_equal, ALU.add)
-        inv_idf = shared.tile([P, PACK], F32, name="inv_idf", align_bytes=64, offset=words_at + T * F32_BYTES // 2)
-        nc.vector.reciprocal(inv_idf[:], idf_or_one[:])
-
-        w2_bf = shared.tile([P, N, PACK], BF16, name="w2_bf", align_bytes=64, offset=words_at)
+        w2_bf = keep.tile([P, N, PACK], BF16, name="w2_bf", tag="word_table", align_bytes=64)
         nc.scalar.copy(
             w2_bf[:, :W2_PIECE, :].rearrange("p (c i) j -> p c j i", i=LINE),
             w2_raw[0][:, :, :W2_PIECE].rearrange("p j (c i) -> p c j i", i=LINE),
@@ -125,22 +126,22 @@ def tile_picked_none_p_kernel(tc, x_words, x_scales, w1, lengths, idf, w2, offs,
             piece = w2_raw[h][:, :, start : start + W2_PIECE].rearrange("p j c -> p c j")
             nc.gpsimd.tensor_scalar(w2_bf[:, col : col + W2_PIECE, :], piece, 1.0, 0.0, ALU.mult, ALU.add)
 
+        groups = [(0, range(0, 1)), (0, range(1, 2)), (0, range(2, 4)), (1, range(0, 2)), (1, range(2, 4))]
         first = {}
-        for h in range(2):
-            for pair in range(2):
-                bank = psum.tile([P, 2, HALF], F32, name=f"first{h}{pair}", tag=f"first{h}{pair}")
-                for e in range(2):
-                    feats = slice((2 * pair + e) * P, (2 * pair + e + 1) * P)
-                    nc.tensor.matmul_mx(
-                        bank[:, e, :],
-                        lhsT=w1_codes[:, feats].bitcast(FP8X4),
-                        lhsT_scale=w1_scale[:, feats],
-                        rhs=x_codes[h][:].bitcast(FP8X4),
-                        rhs_scale=x_scale[:, h * HALF : (h + 1) * HALF],
-                        start=True,
-                        stop=True,
-                    )
-                first[h, pair] = bank
+        for h, planes in groups:
+            bank = psum.tile([P, len(planes), HALF], F32, name=f"first{h}{planes.start}", tag=f"first{h}{planes.start}")
+            for t in planes:
+                feats = slice(t * P, (t + 1) * P)
+                nc.tensor.matmul_mx(
+                    bank[:, t - planes.start, :],
+                    lhsT=w1_codes[:, feats].bitcast(FP8X4),
+                    lhsT_scale=w1_scale[:, feats],
+                    rhs=x_codes[h][:].bitcast(FP8X4),
+                    rhs_scale=x_scale[:, h * HALF : (h + 1) * HALF],
+                    start=True,
+                    stop=True,
+                )
+            first[h, planes] = bank
 
         out_rows = out.rearrange("(b p) s -> p b s", p=P)
         all_places, low, high = slice(0, HALF), slice(0, CHUNK), slice(CHUNK, HALF)
@@ -148,12 +149,6 @@ def tile_picked_none_p_kernel(tc, x_words, x_scales, w1, lengths, idf, w2, offs,
 
         def per_half(name):
             return [keep.tile([P, PACK, HALF], F32, name=f"{name}{h}", align_bytes=64) for h in range(2)]
-
-        def pair_tile(name, h, pair):
-            return keep.tile([P, 2, HALF], F32, name=f"{name}{h}{pair}", tag=f"{name}{h}{pair}", align_bytes=64)
-
-        def plane_of(tiles, h, t):
-            return tiles[h, t // 2][:, t % 2, :]
 
         def chunk_by_lines(tiles, c):
             h, start = divmod(c * CHUNK, HALF)
@@ -170,9 +165,11 @@ def tile_picked_none_p_kernel(tc, x_words, x_scales, w1, lengths, idf, w2, offs,
             w2_scale.append(keep.tile([P, W2_HALF], U8, name=f"w2_scale{h}", align_bytes=64))
             nc.vector.quantize_mx(w2_codes[h][:].bitcast(FP8X4), w2_scale[h][:], w2_bf[:, cols, :].rearrange("p c j -> p (c j)"))
 
-        def make_denominator(h, pair):
-            picked = len_picked[:, 2 * pair : 2 * pair + 2, h * HALF : (h + 1) * HALF]
-            nc.vector.scalar_tensor_tensor(den[h, pair][:], first[h, pair][:], 0.0, picked, ALU.max, ALU.add)
+        def within(tiles, h, planes):
+            return tiles[h, planes.start // 2][:, planes.start % 2 : planes.start % 2 + len(planes), :]
+
+        def make_denominator(h, planes):
+            nc.vector.scalar_tensor_tensor(within(den, h, planes), first[h, planes][:], 0.0, within(picked, h, planes), ALU.max, ALU.add)
 
         def make_root(h, t):
             nc.scalar.activation(plane_of(root, h, t), plane_of(den, h, t), ACT.Abs_reciprocal_sqrt, scale=inv_idf[:, t : t + 1])
@@ -183,9 +180,10 @@ def tile_picked_none_p_kernel(tc, x_words, x_scales, w1, lengths, idf, w2, offs,
         def make_sign(h, t, cols):
             nc.scalar.activation(sign[h][:, t, cols], plane_of(den, h, t)[:, cols], ACT.Sign, scale=idf_sign[:, t : t + 1])
 
-        def make_size(h, pair, cols):
-            planes = slice(2 * pair, 2 * pair + 2)
-            nc.vector.scalar_tensor_tensor(size[h][:, planes, cols], first[h, pair][:, :, cols], 0.0, weight[h, pair][:, :, cols], ALU.max, ALU.mult)
+        def make_size(h, planes, cols):
+            nc.vector.scalar_tensor_tensor(
+                size[h][:, planes.start : planes.stop, cols], first[h, planes][:, :, cols], 0.0, within(weight, h, planes)[:, :, cols], ALU.max, ALU.mult
+            )
 
         def make_z(c):
             woven = z_bf[c][:].rearrange("p (g i) t -> p g t i", i=LINE)
@@ -210,14 +208,17 @@ def tile_picked_none_p_kernel(tc, x_words, x_scales, w1, lengths, idf, w2, offs,
             [(range(0, 4), "second0", "den10")],
             [(range(0, 4), "second1", "den11")],
             [(range(0, 2), "second2", "result20"), (range(2, 4), "first00", "result22")],
-            [(range(b, b + 1), tag, f"result3{b}") for b, tag in enumerate(("second3", "second0", "first10", "first11"))],
+            [(range(b, b + 1), tag, f"result3{b}") for b, tag in enumerate(("first01", "first02", "first10", "first12"))],
         ]
 
-        def project(c):
-            places = slice(c * CHUNK, (c + 1) * CHUNK)
+        def quantise_z(c):
             z_codes = keep.tile([P, CHUNK], U32, name=f"z_codes{c}", align_bytes=64)
             z_scale = keep.tile([P, CHUNK], U8, name=f"z_scale{c}", align_bytes=64)
             nc.vector.quantize_mx(z_codes[:].bitcast(FP8X4), z_scale[:], z_bf[c][:].rearrange("p n t -> p (n t)"))
+            return z_codes, z_scale
+
+        def project(c, z_codes, z_scale):
+            places = slice(c * CHUNK, (c + 1) * CHUNK)
             for blocks, bank_tag, result_tag in exits[c]:
                 bank = second_product(z_codes, z_scale, blocks, bank_tag)
                 result = keep.tile([P, len(blocks), CHUNK], F32, name=f"result{c}{blocks.start}", tag=result_tag, align_bytes=64)
@@ -228,31 +229,25 @@ def tile_picked_none_p_kernel(tc, x_words, x_scales, w1, lengths, idf, w2, offs,
                     nc.scalar.copy(result[:], bank[:])
                 queue = nc.sync if on_vector or c < CHUNKS // 2 else nc.scalar
                 queue.dma_start(out_rows[:, blocks.start : blocks.stop, places], result[:])
-            return z_codes, z_scale
-
-        def warm_up(codes, scale, bank_tag):
-            bank = psum.tile([P, H], F32, name=f"warm_{bank_tag}", tag=bank_tag)
-            nc.tensor.matmul_mx(
-                bank[:], lhsT=codes.bitcast(FP8X4), lhsT_scale=scale, rhs=w1_codes[:].bitcast(FP8X4), rhs_scale=w1_scale[:], start=True, stop=True
-            )
 
         for h in range(2):
             for pair in range(2):
                 den[h, pair] = pair_tile("den", h, pair)
-                make_denominator(h, pair)
-                root[h, pair] = pair_tile("root", h, pair)
+                root[h, pair] = pair_tile("root", h, pair) if h + pair else shared.tile([P, 2, HALF], F32, name="root00", align_bytes=64, offset=0)
                 weight[h, pair] = pair_tile("weight", h, pair)
+        for h, planes in groups:
+            make_denominator(h, planes)
 
+        nc.scalar.activation(plane_of(root, 0, 0), plane_of(den, 0, 0), ACT.Abs_reciprocal_sqrt, scale=0.5)
         make_root(0, 1)
-        nc.scalar.activation(plane_of(root, 0, 0), plane_of(den, 0, 0), ACT.Abs_reciprocal_sqrt, scale=0.25)
+        nc.scalar.activation(sign[0][:, 0, :], plane_of(den, 0, 0), ACT.Sign)
         make_root(0, 2)
         make_root(0, 3)
         make_weight(0, 0, slice(1, 2))
         make_sign(0, 1, all_places)
-        make_sign(0, 2, all_places)
         make_weight(0, 1, both_planes)
+        make_sign(0, 2, all_places)
         make_sign(0, 3, all_places)
-
         for t in range(PACK):
             make_root(1, t)
         make_weight(1, 0, both_planes)
@@ -262,25 +257,22 @@ def tile_picked_none_p_kernel(tc, x_words, x_scales, w1, lengths, idf, w2, offs,
             for t in range(1, PACK):
                 make_sign(1, t, cols)
 
-        quantise_w2(0)
+        make_size(*groups[1], all_places)
         root_0 = plane_of(root, 0, 0)
         nc.vector.scalar_tensor_tensor(plane_of(weight, 0, 0), root_0, idf_sb[:, 0:1], root_0, ALU.mult, ALU.mult)
-        nc.vector.tensor_scalar(sign[0][:, 0, :], plane_of(den, 0, 0), 0.0, 0.5, ALU.is_ge, ALU.subtract)
-
-        make_size(0, 0, all_places)
-        make_size(0, 1, low)
+        quantise_w2(0)
+        make_size(*groups[0], all_places)
+        make_size(*groups[2], low)
         quantise_w2(1)
         make_z(0)
-        make_size(0, 1, high)
-        warm_up(w2_codes[0][:, :P], w2_scale[0][:, :P], "first01")
-        project(0)
+        make_size(*groups[2], high)
+        project(0, *quantise_z(0))
         make_z(1)
-        make_size(1, 0, all_places)
-        chunk_1_codes, chunk_1_scale = project(1)
-        warm_up(chunk_1_codes[:], chunk_1_scale[:], "second3")
-        make_size(1, 1, low)
+        make_size(*groups[3], all_places)
+        project(1, *quantise_z(1))
+        make_size(*groups[4], low)
         make_z(2)
-        make_size(1, 1, high)
-        project(2)
+        make_size(*groups[4], high)
+        project(2, *quantise_z(2))
         make_z(3)
-        project(3)
+        project(3, *quantise_z(3))

@@ -64,7 +64,7 @@ def tile_picked_none_p_kernel(tc, x_words, x_scales, w1, lengths, idf, w2, offs,
         nc.sync.dma_start(offs_sb[:], offs)
         nc.sync.dma_start(len_sb[1][:], len_rows[:, 1, :])
         nc.sync.dma_start(scale_table[0:P:BLOCK_PARTS, :].bitcast(I32), x_scales[0].bitcast(I32))
-        w1_raw = keep.tile([P, PACK, H], F32, name="w1_raw", align_bytes=64)
+        w1_raw = keep.tile([P, PACK, H], F32, name="w1_raw", tag="w1_raw", align_bytes=64)
         nc.sync.dma_start(w1_raw[:], w1.rearrange("(p j) c -> p j c", j=PACK))
         nc.sync.dma_start(len_sb[2][:], len_rows[:, 2, :])
         word_table = keep.tile([P, T], U32, name="word_table", tag="word_table", align_bytes=64)
@@ -73,17 +73,13 @@ def tile_picked_none_p_kernel(tc, x_words, x_scales, w1, lengths, idf, w2, offs,
         scale_picked = keep.tile([P, S], U8, name="scale_picked", align_bytes=64)
         nc.vector.tensor_copy(scale_picked[:], scale_table[:].indirect(offs_sb[:]))
         for e in range(QUADRANT // BLOCK_PARTS):
-            nc.scalar.dma_start(x_scale[e:P:QUADRANT, :].bitcast(I32), scale_picked[BLOCK_PARTS * e : P : QUADRANT, :].bitcast(I32))
+            nc.sync.dma_start(x_scale[e:P:QUADRANT, :].bitcast(I32), scale_picked[BLOCK_PARTS * e : P : QUADRANT, :].bitcast(I32))
 
         len_sb[3] = shared.tile([P, U], F32, name="len_sb3", align_bytes=64, offset=2 * w2_half_bytes)
         nc.sync.dma_start(len_sb[3][:], len_rows[:, 3, :])
 
         idf_sign = keep.tile([P, PACK], F32, name="idf_sign")
         nc.scalar.activation(idf_sign[:], idf_sb[:], ACT.Sign)
-        idf_or_one = keep.tile([P, PACK], F32, name="idf_or_one")
-        nc.vector.scalar_tensor_tensor(idf_or_one[:], idf_sb[:], 0.0, idf_sb[:], ALU.is_equal, ALU.add)
-        inv_idf = keep.tile([P, PACK], F32, name="inv_idf")
-        nc.vector.reciprocal(inv_idf[:], idf_or_one[:])
 
         def pair_tile(name, h, pair):
             return keep.tile([P, 2, HALF], F32, name=f"{name}{h}{pair}", tag=f"{name}{h}{pair}", align_bytes=64)
@@ -92,11 +88,22 @@ def tile_picked_none_p_kernel(tc, x_words, x_scales, w1, lengths, idf, w2, offs,
             return tiles[h, t // 2][:, t % 2, :]
 
         picked = {(h, pair): pair_tile("picked", h, pair) for h in range(2) for pair in range(2)}
-        for t, h in ((0, 0), (0, 1), (1, 0), (1, 1), (2, 0), (2, 1), (3, 0)):
+        def fetch_on_scalar(t, h):
             nc.scalar.activation(plane_of(picked, h, t), len_sb[t][:].indirect(half_of_list(doc_sb, h)), ACT.Copy)
 
-        w1_bf = keep.tile([P, PACK, P, PACK], BF16, name="w1_bf", align_bytes=64)
-        nc.vector.tensor_copy(w1_bf[:].rearrange("p t m j -> p m j t"), w1_raw[:].rearrange("p j (m t) -> p m j t", t=PACK))
+        for t in (0, 1):
+            for h in range(2):
+                fetch_on_scalar(t, h)
+
+        w1_bf = keep.tile([P, PACK, P, PACK], BF16, name="w1_bf", tag="w1_bf", align_bytes=64)
+        for h, cast in enumerate((nc.vector.tensor_copy, nc.scalar.copy)):
+            cast(
+                w1_bf[:, :, h * (P // 2) : (h + 1) * (P // 2), :].rearrange("p t m j -> p m j t"),
+                w1_raw[:, :, h * (H // 2) : (h + 1) * (H // 2)].rearrange("p j (m t) -> p m j t", t=PACK),
+            )
+        nc.vector.tensor_copy(plane_of(picked, 0, 2), len_sb[2][:].indirect(half_of_list(doc_sb, 0)))
+        for t, h in ((2, 1), (3, 0), (3, 1)):
+            fetch_on_scalar(t, h)
 
         w2_rows = w2.rearrange("(p j) c -> p j c", j=PACK)
         w2_raw = []
@@ -109,24 +116,24 @@ def tile_picked_none_p_kernel(tc, x_words, x_scales, w1, lengths, idf, w2, offs,
         w1_scale = keep.tile([P, H], U8, name="w1_scale", align_bytes=64)
         nc.vector.quantize_mx(w1_codes[:].bitcast(FP8X4), w1_scale[:], w1_bf[:].rearrange("p t m j -> p (t m j)"))
 
+        idf_or_one = keep.tile([P, PACK], F32, name="idf_or_one", tag="w1_raw", align_bytes=64)
+        nc.vector.scalar_tensor_tensor(idf_or_one[:], idf_sb[:], 0.0, idf_sb[:], ALU.is_equal, ALU.add)
+        inv_idf = keep.tile([P, PACK], F32, name="inv_idf", tag="w1_bf", align_bytes=64)
+        nc.vector.reciprocal(inv_idf[:], idf_or_one[:])
+
         x_codes = []
         for h in range(2):
             codes = keep.tile([P, HALF], U32, name=f"x_codes{h}", align_bytes=64)
             nc.vector.tensor_copy(codes[:], word_table[:].indirect(half_of_list(offs_sb, h)))
             x_codes.append(codes)
-        nc.vector.tensor_copy(plane_of(picked, 1, 3), len_sb[3][:].indirect(half_of_list(doc_sb, 1)))
 
         w2_bf = keep.tile([P, N, PACK], BF16, name="w2_bf", tag="word_table", align_bytes=64)
-        nc.scalar.copy(
-            w2_bf[:, :W2_PIECE, :].rearrange("p (c i) j -> p c j i", i=LINE),
-            w2_raw[0][:, :, :W2_PIECE].rearrange("p j (c i) -> p c j i", i=LINE),
-        )
-        for col in range(W2_PIECE, N, W2_PIECE):
+        for col in range(0, N, W2_PIECE):
             h, start = divmod(col, W2_HALF)
             piece = w2_raw[h][:, :, start : start + W2_PIECE].rearrange("p j c -> p c j")
             nc.gpsimd.tensor_scalar(w2_bf[:, col : col + W2_PIECE, :], piece, 1.0, 0.0, ALU.mult, ALU.add)
 
-        groups = [(0, range(0, 1)), (0, range(1, 2)), (0, range(2, 4)), (1, range(0, 2)), (1, range(2, 4))]
+        groups = [(0, range(0, 1)), (0, range(1, 2)), (1, range(0, 2)), (0, range(2, 4)), (1, range(2, 4))]
         first = {}
         for h, planes in groups:
             bank = psum.tile([P, len(planes), HALF], F32, name=f"first{h}{planes.start}", tag=f"first{h}{planes.start}")
@@ -161,7 +168,7 @@ def tile_picked_none_p_kernel(tc, x_words, x_scales, w1, lengths, idf, w2, offs,
 
         def quantise_w2(h):
             cols = slice(h * W2_HALF, (h + 1) * W2_HALF)
-            w2_codes.append(keep.tile([P, W2_HALF], U32, name=f"w2_codes{h}", align_bytes=64))
+            w2_codes.append(keep.tile([P, W2_HALF], U32, name=f"w2_codes{h}", tag=("picked01", "picked11")[h], align_bytes=64))
             w2_scale.append(keep.tile([P, W2_HALF], U8, name=f"w2_scale{h}", align_bytes=64))
             nc.vector.quantize_mx(w2_codes[h][:].bitcast(FP8X4), w2_scale[h][:], w2_bf[:, cols, :].rearrange("p c j -> p (c j)"))
 
@@ -174,8 +181,8 @@ def tile_picked_none_p_kernel(tc, x_words, x_scales, w1, lengths, idf, w2, offs,
         def make_root(h, t):
             nc.scalar.activation(plane_of(root, h, t), plane_of(den, h, t), ACT.Abs_reciprocal_sqrt, scale=inv_idf[:, t : t + 1])
 
-        def make_weight(h, pair, planes):
-            nc.scalar.activation(weight[h, pair][:, planes, :], root[h, pair][:, planes, :], ACT.Square, scale=math.sqrt(2.0))
+        def make_weight(h, pair, planes, cols=slice(0, HALF)):
+            nc.scalar.activation(weight[h, pair][:, planes, cols], root[h, pair][:, planes, cols], ACT.Square, scale=math.sqrt(2.0))
 
         def make_sign(h, t, cols):
             nc.scalar.activation(sign[h][:, t, cols], plane_of(den, h, t)[:, cols], ACT.Sign, scale=idf_sign[:, t : t + 1])
@@ -185,9 +192,10 @@ def tile_picked_none_p_kernel(tc, x_words, x_scales, w1, lengths, idf, w2, offs,
                 size[h][:, planes.start : planes.stop, cols], first[h, planes][:, :, cols], 0.0, within(weight, h, planes)[:, :, cols], ALU.max, ALU.mult
             )
 
-        def make_z(c):
-            woven = z_bf[c][:].rearrange("p (g i) t -> p g t i", i=LINE)
-            nc.vector.tensor_tensor(woven, chunk_by_lines(size, c), chunk_by_lines(sign, c), ALU.mult)
+        def make_z(c, part=slice(0, CHUNK)):
+            groups_of_four = slice(part.start // LINE, part.stop // LINE)
+            woven = z_bf[c][:, part, :].rearrange("p (g i) t -> p g t i", i=LINE)
+            nc.vector.tensor_tensor(woven, chunk_by_lines(size, c)[:, groups_of_four], chunk_by_lines(sign, c)[:, groups_of_four], ALU.mult)
 
         def second_product(z_codes, z_scale, blocks, bank_tag):
             bank = psum.tile([P, len(blocks), CHUNK], F32, name=bank_tag, tag=bank_tag)
@@ -205,24 +213,25 @@ def tile_picked_none_p_kernel(tc, x_words, x_scales, w1, lengths, idf, w2, offs,
             return bank
 
         exits = [
-            [(range(0, 4), "second0", "den10")],
-            [(range(0, 4), "second1", "den11")],
-            [(range(0, 2), "second2", "result20"), (range(2, 4), "first00", "result22")],
-            [(range(b, b + 1), tag, f"result3{b}") for b, tag in enumerate(("first01", "first02", "first10", "first12"))],
+            [(range(0, 4), "second0", "den10", nc.scalar)],
+            [(range(0, 4), "second1", "den11", nc.scalar)],
+            [(range(0, 2), "second2", "result20", nc.scalar), (range(2, 4), "first00", "result22", nc.scalar)],
+            [(range(b, b + 1), tag, f"result3{b}", (nc.vector, nc.scalar)[b % 2]) for b, tag in enumerate(("first01", "first02", "first10", "first12"))],
         ]
 
-        def quantise_z(c):
+        def quantise_z(c, parts=(slice(0, CHUNK),)):
             z_codes = keep.tile([P, CHUNK], U32, name=f"z_codes{c}", align_bytes=64)
             z_scale = keep.tile([P, CHUNK], U8, name=f"z_scale{c}", align_bytes=64)
-            nc.vector.quantize_mx(z_codes[:].bitcast(FP8X4), z_scale[:], z_bf[c][:].rearrange("p n t -> p (n t)"))
+            for part in parts:
+                nc.vector.quantize_mx(z_codes[:, part].bitcast(FP8X4), z_scale[:, part], z_bf[c][:, part, :].rearrange("p n t -> p (n t)"))
             return z_codes, z_scale
 
         def project(c, z_codes, z_scale):
             places = slice(c * CHUNK, (c + 1) * CHUNK)
-            for blocks, bank_tag, result_tag in exits[c]:
+            for blocks, bank_tag, result_tag, engine in exits[c]:
                 bank = second_product(z_codes, z_scale, blocks, bank_tag)
                 result = keep.tile([P, len(blocks), CHUNK], F32, name=f"result{c}{blocks.start}", tag=result_tag, align_bytes=64)
-                on_vector = c == CHUNKS - 1 and blocks.stop < ROW_BLOCKS
+                on_vector = engine is nc.vector
                 if on_vector:
                     nc.vector.tensor_copy(result[:], bank[:])
                 else:
@@ -233,46 +242,55 @@ def tile_picked_none_p_kernel(tc, x_words, x_scales, w1, lengths, idf, w2, offs,
         for h in range(2):
             for pair in range(2):
                 den[h, pair] = pair_tile("den", h, pair)
-                root[h, pair] = pair_tile("root", h, pair) if h + pair else shared.tile([P, 2, HALF], F32, name="root00", align_bytes=64, offset=0)
                 weight[h, pair] = pair_tile("weight", h, pair)
         for h, planes in groups:
             make_denominator(h, planes)
 
-        nc.scalar.activation(plane_of(root, 0, 0), plane_of(den, 0, 0), ACT.Abs_reciprocal_sqrt, scale=0.5)
+        root[0, 0] = pair_tile("root", 0, 0)
+        root[0, 1] = pair_tile("root", 0, 1)
+        make_root(0, 0)
         make_root(0, 1)
-        nc.scalar.activation(sign[0][:, 0, :], plane_of(den, 0, 0), ACT.Sign)
+        make_sign(0, 0, all_places)
+        make_weight(0, 0, both_planes)
         make_root(0, 2)
         make_root(0, 3)
-        make_weight(0, 0, slice(1, 2))
         make_sign(0, 1, all_places)
         make_weight(0, 1, both_planes)
         make_sign(0, 2, all_places)
         make_sign(0, 3, all_places)
-        for t in range(PACK):
-            make_root(1, t)
-        make_weight(1, 0, both_planes)
+        root[1, 0] = keep.tile([P, 2, HALF], F32, name="root10", tag="root01", align_bytes=64)
+        root[1, 1] = keep.tile([P, 2, HALF], F32, name="root11", tag="den01", align_bytes=64)
+        make_root(1, 0)
+        nc.scalar.activation(plane_of(root, 1, 1), plane_of(den, 1, 1), ACT.Abs_reciprocal_sqrt, scale=0.5)
+        make_root(1, 2)
+        make_weight(1, 0, slice(0, 1))
+        make_root(1, 3)
         make_sign(1, 0, all_places)
-        make_weight(1, 1, both_planes)
         for cols in (low, high):
-            for t in range(1, PACK):
+            make_weight(1, 1, both_planes, cols)
+            nc.scalar.activation(sign[1][:, 1, cols], plane_of(den, 1, 1)[:, cols], ACT.Sign)
+            for t in range(2, PACK):
                 make_sign(1, t, cols)
 
-        make_size(*groups[1], all_places)
-        root_0 = plane_of(root, 0, 0)
-        nc.vector.scalar_tensor_tensor(plane_of(weight, 0, 0), root_0, idf_sb[:, 0:1], root_0, ALU.mult, ALU.mult)
-        quantise_w2(0)
         make_size(*groups[0], all_places)
-        make_size(*groups[2], low)
+        make_size(*groups[1], all_places)
+        quantise_w2(0)
         quantise_w2(1)
+        make_size(*groups[3], low)
+        make_size(*groups[3], high)
         make_z(0)
-        make_size(*groups[2], high)
-        project(0, *quantise_z(0))
         make_z(1)
-        make_size(*groups[3], all_places)
+        project(0, *quantise_z(0))
+        root_1 = plane_of(root, 1, 1)
+        nc.vector.scalar_tensor_tensor(plane_of(weight, 1, 1), root_1, idf_sb[:, 1:2], root_1, ALU.mult, ALU.mult)
         project(1, *quantise_z(1))
+        make_size(*groups[2], low)
         make_size(*groups[4], low)
+        make_size(*groups[2], high)
         make_z(2)
         make_size(*groups[4], high)
         project(2, *quantise_z(2))
-        make_z(3)
-        project(3, *quantise_z(3))
+        halves = (slice(0, CHUNK // 2), slice(CHUNK // 2, CHUNK))
+        for part in halves:
+            make_z(3, part)
+        project(3, *quantise_z(3, halves))

@@ -28,6 +28,7 @@ HALF = S // 2
 W2_HALF = N // 2
 W2_PIECE = N // 4
 PLANE_BYTES = U * 4
+WARM_ROWS = 32
 LINE = 4
 
 
@@ -132,6 +133,21 @@ def tile_picked_none_p_kernel(tc, x_words, x_scales, w1, lengths, idf, w2, offs,
             h, start = divmod(col, W2_HALF)
             piece = w2_raw[h][:, :, start : start + W2_PIECE].rearrange("p j c -> p c j")
             nc.gpsimd.tensor_scalar(w2_bf[:, col : col + W2_PIECE, :], piece, 1.0, 0.0, ALU.mult, ALU.add)
+
+        def warm_up(codes, scale, bank_tag):
+            bank = psum.tile([WARM_ROWS, H], F32, name=f"warm_{bank_tag}", tag=bank_tag)
+            nc.tensor.matmul_mx(
+                bank[:],
+                lhsT=codes[:, :WARM_ROWS].bitcast(FP8X4),
+                lhsT_scale=scale[:, :WARM_ROWS],
+                rhs=w1_codes[:].bitcast(FP8X4),
+                rhs_scale=w1_scale[:],
+                start=True,
+                stop=True,
+            )
+
+        warm_up(w1_codes, w1_scale, "second0")
+        warm_up(w1_codes, w1_scale, "second1")
 
         groups = [(0, range(0, 1)), (0, range(1, 2)), (1, range(0, 2)), (0, range(2, 4)), (1, range(2, 4))]
         first = {}
@@ -283,7 +299,9 @@ def tile_picked_none_p_kernel(tc, x_words, x_scales, w1, lengths, idf, w2, offs,
         project(0, *quantise_z(0))
         root_1 = plane_of(root, 1, 1)
         nc.vector.scalar_tensor_tensor(plane_of(weight, 1, 1), root_1, idf_sb[:, 1:2], root_1, ALU.mult, ALU.mult)
-        project(1, *quantise_z(1))
+        chunk_1 = quantise_z(1)
+        project(1, *chunk_1)
+        warm_up(*chunk_1, "second2")
         make_size(*groups[2], low)
         make_size(*groups[4], low)
         make_size(*groups[2], high)

@@ -29,6 +29,7 @@ W2_HALF = N // 2
 W2_PIECE = N // 4
 PLANE_BYTES = U * 4
 WARM_ROWS = 32
+ALIGN = 256
 LINE = 4
 
 
@@ -52,38 +53,38 @@ def tile_picked_none_p_kernel(tc, x_words, x_scales, w1, lengths, idf, w2, offs,
         nc.scalar.activation(warm[:, 1:2], warm[:, 0:1], ACT.Abs_reciprocal_sqrt)
 
         w2_half_bytes = PACK * W2_HALF * 4
-        scale_table = shared.tile([P, T], U8, name="scale_table", align_bytes=64, offset=2 * w2_half_bytes)
+        scale_table = shared.tile([P, T], U8, name="scale_table", align_bytes=ALIGN, offset=2 * w2_half_bytes)
         nc.vector.memset(scale_table[:].bitcast(I32), 0)
-        x_scale = keep.tile([P, S], U8, name="x_scale", align_bytes=64)
+        x_scale = keep.tile([P, S], U8, name="x_scale", align_bytes=ALIGN)
         nc.gpsimd.memset(x_scale[:].bitcast(I32), 0)
 
         len_rows = lengths.rearrange("(p t) u -> p t u", t=PACK)
-        len_sb = {t: keep.tile([P, U], F32, name=f"len_sb{t}", align_bytes=64) for t in (1, 2)}
-        len_sb[0] = shared.tile([P, U], F32, name="len_sb0", align_bytes=64, offset=w2_half_bytes - PLANE_BYTES // 2)
+        len_sb = {t: keep.tile([P, U], F32, name=f"len_sb{t}", align_bytes=ALIGN) for t in (1, 2)}
+        len_sb[0] = shared.tile([P, U], F32, name="len_sb0", align_bytes=ALIGN, offset=w2_half_bytes - PLANE_BYTES // 2)
         nc.sync.dma_start(len_sb[0][:], len_rows[:, 0, :])
         nc.sync.dma_start(doc_sb[:], doc)
         nc.sync.dma_start(offs_sb[:], offs)
         nc.sync.dma_start(len_sb[1][:], len_rows[:, 1, :])
         nc.sync.dma_start(scale_table[0:P:BLOCK_PARTS, :].bitcast(I32), x_scales[0].bitcast(I32))
-        w1_raw = keep.tile([P, PACK, H], F32, name="w1_raw", tag="w1_raw", align_bytes=64)
+        w1_raw = keep.tile([P, PACK, H], F32, name="w1_raw", tag="w1_raw", align_bytes=ALIGN)
         nc.sync.dma_start(w1_raw[:], w1.rearrange("(p j) c -> p j c", j=PACK))
         nc.sync.dma_start(len_sb[2][:], len_rows[:, 2, :])
-        word_table = keep.tile([P, T], U32, name="word_table", tag="word_table", align_bytes=64)
+        word_table = keep.tile([P, T], U32, name="word_table", tag="word_table", align_bytes=ALIGN)
         nc.sync.dma_start(word_table[:].bitcast(I32), x_words[0].rearrange("p n r -> p (n r)").bitcast(I32))
 
-        scale_picked = keep.tile([P, S], U8, name="scale_picked", align_bytes=64)
+        scale_picked = keep.tile([P, S], U8, name="scale_picked", align_bytes=ALIGN)
         nc.vector.tensor_copy(scale_picked[:], scale_table[:].indirect(offs_sb[:]))
         for e in range(QUADRANT // BLOCK_PARTS):
             nc.sync.dma_start(x_scale[e:P:QUADRANT, :].bitcast(I32), scale_picked[BLOCK_PARTS * e : P : QUADRANT, :].bitcast(I32))
 
-        len_sb[3] = shared.tile([P, U], F32, name="len_sb3", align_bytes=64, offset=2 * w2_half_bytes)
+        len_sb[3] = shared.tile([P, U], F32, name="len_sb3", align_bytes=ALIGN, offset=2 * w2_half_bytes)
         nc.sync.dma_start(len_sb[3][:], len_rows[:, 3, :])
 
         idf_sign = keep.tile([P, PACK], F32, name="idf_sign")
         nc.scalar.activation(idf_sign[:], idf_sb[:], ACT.Sign)
 
         def pair_tile(name, h, pair):
-            return keep.tile([P, 2, HALF], F32, name=f"{name}{h}{pair}", tag=f"{name}{h}{pair}", align_bytes=64)
+            return keep.tile([P, 2, HALF], F32, name=f"{name}{h}{pair}", tag=f"{name}{h}{pair}", align_bytes=ALIGN)
 
         def plane_of(tiles, h, t):
             return tiles[h, t // 2][:, t % 2, :]
@@ -96,7 +97,7 @@ def tile_picked_none_p_kernel(tc, x_words, x_scales, w1, lengths, idf, w2, offs,
             for h in range(2):
                 fetch_on_scalar(t, h)
 
-        w1_bf = keep.tile([P, PACK, P, PACK], BF16, name="w1_bf", tag="w1_bf", align_bytes=64)
+        w1_bf = keep.tile([P, PACK, P, PACK], BF16, name="w1_bf", tag="w1_bf", align_bytes=ALIGN)
         for h, cast in enumerate((nc.vector.tensor_copy, nc.scalar.copy)):
             cast(
                 w1_bf[:, :, h * (P // 2) : (h + 1) * (P // 2), :].rearrange("p t m j -> p m j t"),
@@ -109,26 +110,26 @@ def tile_picked_none_p_kernel(tc, x_words, x_scales, w1, lengths, idf, w2, offs,
         w2_rows = w2.rearrange("(p j) c -> p j c", j=PACK)
         w2_raw = []
         for h in range(2):
-            raw = shared.tile([P, PACK, W2_HALF], F32, name=f"w2_raw{h}", align_bytes=64, offset=h * w2_half_bytes)
+            raw = shared.tile([P, PACK, W2_HALF], F32, name=f"w2_raw{h}", align_bytes=ALIGN, offset=h * w2_half_bytes)
             nc.sync.dma_start(raw[:], w2_rows[:, :, h * W2_HALF : (h + 1) * W2_HALF])
             w2_raw.append(raw)
 
-        w1_codes = keep.tile([P, H], U32, name="w1_codes", align_bytes=64)
-        w1_scale = keep.tile([P, H], U8, name="w1_scale", align_bytes=64)
+        w1_codes = keep.tile([P, H], U32, name="w1_codes", align_bytes=ALIGN)
+        w1_scale = keep.tile([P, H], U8, name="w1_scale", align_bytes=ALIGN)
         nc.vector.quantize_mx(w1_codes[:].bitcast(FP8X4), w1_scale[:], w1_bf[:].rearrange("p t m j -> p (t m j)"))
 
-        idf_or_one = keep.tile([P, PACK], F32, name="idf_or_one", tag="w1_raw", align_bytes=64)
+        idf_or_one = keep.tile([P, PACK], F32, name="idf_or_one", tag="w1_raw", align_bytes=ALIGN)
         nc.vector.scalar_tensor_tensor(idf_or_one[:], idf_sb[:], 0.0, idf_sb[:], ALU.is_equal, ALU.add)
-        inv_idf = keep.tile([P, PACK], F32, name="inv_idf", tag="w1_bf", align_bytes=64)
+        inv_idf = keep.tile([P, PACK], F32, name="inv_idf", tag="w1_bf", align_bytes=ALIGN)
         nc.vector.reciprocal(inv_idf[:], idf_or_one[:])
 
         x_codes = []
         for h in range(2):
-            codes = keep.tile([P, HALF], U32, name=f"x_codes{h}", align_bytes=64)
+            codes = keep.tile([P, HALF], U32, name=f"x_codes{h}", align_bytes=ALIGN)
             nc.vector.tensor_copy(codes[:], word_table[:].indirect(half_of_list(offs_sb, h)))
             x_codes.append(codes)
 
-        w2_bf = keep.tile([P, N, PACK], BF16, name="w2_bf", tag="word_table", align_bytes=64)
+        w2_bf = keep.tile([P, N, PACK], BF16, name="w2_bf", tag="word_table", align_bytes=ALIGN)
         for col in range(0, N, W2_PIECE):
             h, start = divmod(col, W2_HALF)
             piece = w2_raw[h][:, :, start : start + W2_PIECE].rearrange("p j c -> p c j")
@@ -171,7 +172,7 @@ def tile_picked_none_p_kernel(tc, x_words, x_scales, w1, lengths, idf, w2, offs,
         both_planes = slice(0, 2)
 
         def per_half(name):
-            return [keep.tile([P, PACK, HALF], F32, name=f"{name}{h}", align_bytes=64) for h in range(2)]
+            return [keep.tile([P, PACK, HALF], F32, name=f"{name}{h}", align_bytes=ALIGN) for h in range(2)]
 
         def chunk_by_lines(tiles, c):
             h, start = divmod(c * CHUNK, HALF)
@@ -179,13 +180,13 @@ def tile_picked_none_p_kernel(tc, x_words, x_scales, w1, lengths, idf, w2, offs,
 
         sign, size = per_half("sign"), per_half("size")
         den, root, weight = {}, {}, {}
-        z_bf = [keep.tile([P, CHUNK, PACK], BF16, name=f"z_bf{c}", align_bytes=64) for c in range(CHUNKS)]
+        z_bf = [keep.tile([P, CHUNK, PACK], BF16, name=f"z_bf{c}", align_bytes=ALIGN) for c in range(CHUNKS)]
         w2_codes, w2_scale = [], []
 
         def quantise_w2(h):
             cols = slice(h * W2_HALF, (h + 1) * W2_HALF)
-            w2_codes.append(keep.tile([P, W2_HALF], U32, name=f"w2_codes{h}", tag=("picked01", "picked11")[h], align_bytes=64))
-            w2_scale.append(keep.tile([P, W2_HALF], U8, name=f"w2_scale{h}", align_bytes=64))
+            w2_codes.append(keep.tile([P, W2_HALF], U32, name=f"w2_codes{h}", tag=("picked01", "picked11")[h], align_bytes=ALIGN))
+            w2_scale.append(keep.tile([P, W2_HALF], U8, name=f"w2_scale{h}", align_bytes=ALIGN))
             nc.vector.quantize_mx(w2_codes[h][:].bitcast(FP8X4), w2_scale[h][:], w2_bf[:, cols, :].rearrange("p c j -> p (c j)"))
 
         def within(tiles, h, planes):
@@ -236,8 +237,8 @@ def tile_picked_none_p_kernel(tc, x_words, x_scales, w1, lengths, idf, w2, offs,
         ]
 
         def quantise_z(c, parts=(slice(0, CHUNK),)):
-            z_codes = keep.tile([P, CHUNK], U32, name=f"z_codes{c}", align_bytes=64)
-            z_scale = keep.tile([P, CHUNK], U8, name=f"z_scale{c}", align_bytes=64)
+            z_codes = keep.tile([P, CHUNK], U32, name=f"z_codes{c}", align_bytes=ALIGN)
+            z_scale = keep.tile([P, CHUNK], U8, name=f"z_scale{c}", align_bytes=ALIGN)
             for part in parts:
                 nc.vector.quantize_mx(z_codes[:, part].bitcast(FP8X4), z_scale[:, part], z_bf[c][:, part, :].rearrange("p n t -> p (n t)"))
             return z_codes, z_scale
@@ -246,7 +247,7 @@ def tile_picked_none_p_kernel(tc, x_words, x_scales, w1, lengths, idf, w2, offs,
             places = slice(c * CHUNK, (c + 1) * CHUNK)
             for blocks, bank_tag, result_tag, engine in exits[c]:
                 bank = second_product(z_codes, z_scale, blocks, bank_tag)
-                result = keep.tile([P, len(blocks), CHUNK], F32, name=f"result{c}{blocks.start}", tag=result_tag, align_bytes=64)
+                result = keep.tile([P, len(blocks), CHUNK], F32, name=f"result{c}{blocks.start}", tag=result_tag, align_bytes=ALIGN)
                 on_vector = engine is nc.vector
                 if on_vector:
                     nc.vector.tensor_copy(result[:], bank[:])
@@ -274,8 +275,8 @@ def tile_picked_none_p_kernel(tc, x_words, x_scales, w1, lengths, idf, w2, offs,
         make_weight(0, 1, both_planes)
         make_sign(0, 2, all_places)
         make_sign(0, 3, all_places)
-        root[1, 0] = keep.tile([P, 2, HALF], F32, name="root10", tag="root01", align_bytes=64)
-        root[1, 1] = keep.tile([P, 2, HALF], F32, name="root11", tag="den01", align_bytes=64)
+        root[1, 0] = keep.tile([P, 2, HALF], F32, name="root10", tag="root01", align_bytes=ALIGN)
+        root[1, 1] = keep.tile([P, 2, HALF], F32, name="root11", tag="den01", align_bytes=ALIGN)
         make_root(1, 0)
         nc.scalar.activation(plane_of(root, 1, 1), plane_of(den, 1, 1), ACT.Abs_reciprocal_sqrt, scale=0.5)
         make_root(1, 2)

@@ -277,16 +277,12 @@ def tile_picked_none_p_kernel(tc, x_words, x_scales, w1, lengths, idf, w2, offs,
         make_sign(0, 3, all_places)
         root[1, 0] = keep.tile([P, 2, HALF], F32, name="root10", tag="root01", align_bytes=ALIGN)
         root[1, 1] = keep.tile([P, 2, HALF], F32, name="root11", tag="den01", align_bytes=ALIGN)
-        make_root(1, 0)
-        nc.scalar.activation(plane_of(root, 1, 1), plane_of(den, 1, 1), ACT.Abs_reciprocal_sqrt, scale=0.5)
-        make_root(1, 2)
-        make_weight(1, 0, slice(0, 1))
-        make_root(1, 3)
-        make_sign(1, 0, all_places)
+        for t in range(PACK):
+            make_root(1, t)
         for cols in (low, high):
-            make_weight(1, 1, both_planes, cols)
-            nc.scalar.activation(sign[1][:, 1, cols], plane_of(den, 1, 1)[:, cols], ACT.Sign)
-            for t in range(2, PACK):
+            for pair in range(2):
+                make_weight(1, pair, both_planes, cols)
+            for t in range(PACK):
                 make_sign(1, t, cols)
 
         make_size(*groups[0], all_places)
@@ -298,15 +294,13 @@ def tile_picked_none_p_kernel(tc, x_words, x_scales, w1, lengths, idf, w2, offs,
         make_z(0)
         make_z(1)
         project(0, *quantise_z(0))
-        root_1 = plane_of(root, 1, 1)
-        nc.vector.scalar_tensor_tensor(plane_of(weight, 1, 1), root_1, idf_sb[:, 1:2], root_1, ALU.mult, ALU.mult)
         chunk_1 = quantise_z(1)
         project(1, *chunk_1)
         warm_up(*chunk_1, "second2")
         make_size(*groups[2], low)
         make_size(*groups[4], low)
-        make_size(*groups[2], high)
         make_z(2)
+        make_size(*groups[2], high)
         make_size(*groups[4], high)
         project(2, *quantise_z(2))
         halves = (slice(0, CHUNK // 2), slice(CHUNK // 2, CHUNK))

@@ -26,7 +26,7 @@ CHUNKS = S // CHUNK
 ROW_BLOCKS = N // P
 HALF = S // 2
 W2_HALF = N // 2
-W2_PIECE = N // 4
+W2_PIECE = N // 2
 PLANE_BYTES = U * 4
 WARM_ROWS = 32
 ALIGN = 256

import math
from contextlib import ExitStack

import concourse.mybir as mybir

K, T, S, N, H, U = 512, 2048, 512, 512, 512, 512
FLOPS = 2 * K * H * S + 2 * H * N * S

F32 = mybir.dt.float32
BF16 = mybir.dt.bfloat16
I32 = mybir.dt.int32
U32 = mybir.dt.uint32
U16 = mybir.dt.uint16
U8 = mybir.dt.uint8
FP8X4 = mybir.dt.float8_e4m3fn_x4
ALU = mybir.AluOpType
ACT = mybir.ActivationFunctionType

P = 128
PACK = 4
BLOCK_PARTS = 8
QUADRANT = 32
PER_COL = 16
CHUNK = 128
CHUNKS = S // CHUNK
ROW_BLOCKS = N // P
HALF = S // 2
W2_HALF = N // 2
W2_PIECE = N // 2
PLANE_BYTES = U * 4
WARM_ROWS = 32
ALIGN = 256
LINE = 4


def tile_picked_none_p_kernel(tc, x_words, x_scales, w1, lengths, idf, w2, offs, doc, out):
    nc = tc.nc
    with ExitStack() as ctx:
        keep = ctx.enter_context(tc.tile_pool(name="keep", bufs=1))
        shared = ctx.enter_context(tc.tile_pool(name="shared", bufs=1))
        psum = ctx.enter_context(tc.psum_pool(name="psum", bufs=1))

        def half_of_list(list_tile, h):
            return list_tile[:, h * HALF // PER_COL : (h + 1) * HALF // PER_COL]

        offs_sb = keep.tile([P, S // PER_COL], U16, name="offs_sb")
        doc_sb = keep.tile([P, S // PER_COL], U16, name="doc_sb")
        idf_sb = keep.tile([P, PACK], F32, name="idf_sb")
        nc.scalar.dma_start(idf_sb[:], idf.rearrange("(p t) o -> p (t o)", t=PACK))

        warm = keep.tile([P, 2], F32, name="warm")
        nc.vector.memset(warm[:, 0:1], 1.0)
        nc.scalar.activation(warm[:, 1:2], warm[:, 0:1], ACT.Abs_reciprocal_sqrt)

        w2_half_bytes = PACK * W2_HALF * 4
        scale_table = shared.tile([P, T], U8, name="scale_table", align_bytes=ALIGN, offset=2 * w2_half_bytes)
        nc.vector.memset(scale_table[:].bitcast(I32), 0)
        x_scale = keep.tile([P, S], U8, name="x_scale", align_bytes=ALIGN)
        nc.gpsimd.memset(x_scale[:].bitcast(I32), 0)

        len_rows = lengths.rearrange("(p t) u -> p t u", t=PACK)
        len_sb = {t: keep.tile([P, U], F32, name=f"len_sb{t}", align_bytes=ALIGN) for t in (1, 2)}
        len_sb[0] = shared.tile([P, U], F32, name="len_sb0", align_bytes=ALIGN, offset=w2_half_bytes - PLANE_BYTES // 2)
        nc.sync.dma_start(len_sb[0][:], len_rows[:, 0, :])
        nc.sync.dma_start(doc_sb[:], doc)
        nc.sync.dma_start(offs_sb[:], offs)
        nc.sync.dma_start(len_sb[1][:], len_rows[:, 1, :])
        nc.sync.dma_start(scale_table[0:P:BLOCK_PARTS, :].bitcast(I32), x_scales[0].bitcast(I32))
        w1_raw = keep.tile([P, PACK, H], F32, name="w1_raw", tag="w1_raw", align_bytes=ALIGN)
        nc.sync.dma_start(w1_raw[:], w1.rearrange("(p j) c -> p j c", j=PACK))
        nc.sync.dma_start(len_sb[2][:], len_rows[:, 2, :])
        word_table = keep.tile([P, T], U32, name="word_table", tag="word_table", align_bytes=ALIGN)
        nc.sync.dma_start(word_table[:].bitcast(I32), x_words[0].rearrange("p n r -> p (n r)").bitcast(I32))

        scale_picked = keep.tile([P, S], U8, name="scale_picked", align_bytes=ALIGN)
        nc.vector.tensor_copy(scale_picked[:], scale_table[:].indirect(offs_sb[:]))
        for e in range(QUADRANT // BLOCK_PARTS):
            nc.sync.dma_start(x_scale[e:P:QUADRANT, :].bitcast(I32), scale_picked[BLOCK_PARTS * e : P : QUADRANT, :].bitcast(I32))

        len_sb[3] = shared.tile([P, U], F32, name="len_sb3", align_bytes=ALIGN, offset=2 * w2_half_bytes)
        nc.sync.dma_start(len_sb[3][:], len_rows[:, 3, :])

        idf_sign = keep.tile([P, PACK], F32, name="idf_sign")
        nc.scalar.activation(idf_sign[:], idf_sb[:], ACT.Sign)

        def pair_tile(name, h, pair):
            return keep.tile([P, 2, HALF], F32, name=f"{name}{h}{pair}", tag=f"{name}{h}{pair}", align_bytes=ALIGN)

        def plane_of(tiles, h, t):
            return tiles[h, t // 2][:, t % 2, :]

        picked = {(h, pair): pair_tile("picked", h, pair) for h in range(2) for pair in range(2)}
        def fetch_on_scalar(t, h):
            nc.scalar.activation(plane_of(picked, h, t), len_sb[t][:].indirect(half_of_list(doc_sb, h)), ACT.Copy)

        for t in (0, 1):
            for h in range(2):
                fetch_on_scalar(t, h)

        w1_bf = keep.tile([P, PACK, P, PACK], BF16, name="w1_bf", tag="w1_bf", align_bytes=ALIGN)
        for h, cast in enumerate((nc.vector.tensor_copy, nc.scalar.copy)):
            cast(
                w1_bf[:, :, h * (P // 2) : (h + 1) * (P // 2), :].rearrange("p t m j -> p m j t"),
                w1_raw[:, :, h * (H // 2) : (h + 1) * (H // 2)].rearrange("p j (m t) -> p m j t", t=PACK),
            )
        nc.vector.tensor_copy(plane_of(picked, 0, 2), len_sb[2][:].indirect(half_of_list(doc_sb, 0)))
        for t, h in ((2, 1), (3, 0), (3, 1)):
            fetch_on_scalar(t, h)

        w2_rows = w2.rearrange("(p j) c -> p j c", j=PACK)
        w2_raw = []
        for h in range(2):
            raw = shared.tile([P, PACK, W2_HALF], F32, name=f"w2_raw{h}", align_bytes=ALIGN, offset=h * w2_half_bytes)
            nc.sync.dma_start(raw[:], w2_rows[:, :, h * W2_HALF : (h + 1) * W2_HALF])
            w2_raw.append(raw)

        w1_codes = keep.tile([P, H], U32, name="w1_codes", align_bytes=ALIGN)
        w1_scale = keep.tile([P, H], U8, name="w1_scale", align_bytes=ALIGN)
        nc.vector.quantize_mx(w1_codes[:].bitcast(FP8X4), w1_scale[:], w1_bf[:].rearrange("p t m j -> p (t m j)"))

        idf_or_one = keep.tile([P, PACK], F32, name="idf_or_one", tag="w1_raw", align_bytes=ALIGN)
        nc.vector.scalar_tensor_tensor(idf_or_one[:], idf_sb[:], 0.0, idf_sb[:], ALU.is_equal, ALU.add)
        inv_idf = keep.tile([P, PACK], F32, name="inv_idf", tag="w1_bf", align_bytes=ALIGN)
        nc.vector.reciprocal(inv_idf[:], idf_or_one[:])

        x_codes = []
        for h in range(2):
            codes = keep.tile([P, HALF], U32, name=f"x_codes{h}", align_bytes=ALIGN)
            nc.vector.tensor_copy(codes[:], word_table[:].indirect(half_of_list(offs_sb, h)))
            x_codes.append(codes)

        w2_bf = keep.tile([P, N, PACK], BF16, name="w2_bf", tag="word_table", align_bytes=ALIGN)
        for col in range(0, N, W2_PIECE):
            h, start = divmod(col, W2_HALF)
            piece = w2_raw[h][:, :, start : start + W2_PIECE].rearrange("p j c -> p c j")
            nc.gpsimd.tensor_scalar(w2_bf[:, col : col + W2_PIECE, :], piece, 1.0, 0.0, ALU.mult, ALU.add)

        def warm_up(codes, scale, bank_tag):
            bank = psum.tile([WARM_ROWS, H], F32, name=f"warm_{bank_tag}", tag=bank_tag)
            nc.tensor.matmul_mx(
                bank[:],
                lhsT=codes[:, :WARM_ROWS].bitcast(FP8X4),
                lhsT_scale=scale[:, :WARM_ROWS],
                rhs=w1_codes[:].bitcast(FP8X4),
                rhs_scale=w1_scale[:],
                start=True,
                stop=True,
            )

        warm_up(w1_codes, w1_scale, "second0")
        warm_up(w1_codes, w1_scale, "second1")

        groups = [(0, range(0, 1)), (0, range(1, 2)), (1, range(0, 2)), (0, range(2, 4)), (1, range(2, 4))]
        first = {}
        for h, planes in groups:
            bank = psum.tile([P, len(planes), HALF], F32, name=f"first{h}{planes.start}", tag=f"first{h}{planes.start}")
            for t in planes:
                feats = slice(t * P, (t + 1) * P)
                nc.tensor.matmul_mx(
                    bank[:, t - planes.start, :],
                    lhsT=w1_codes[:, feats].bitcast(FP8X4),
                    lhsT_scale=w1_scale[:, feats],
                    rhs=x_codes[h][:].bitcast(FP8X4),
                    rhs_scale=x_scale[:, h * HALF : (h + 1) * HALF],
                    start=True,
                    stop=True,
                )
            first[h, planes] = bank

        out_rows = out.rearrange("(b p) s -> p b s", p=P)
        all_places, low, high = slice(0, HALF), slice(0, CHUNK), slice(CHUNK, HALF)
        both_planes = slice(0, 2)

        def per_half(name):
            return [keep.tile([P, PACK, HALF], F32, name=f"{name}{h}", align_bytes=ALIGN) for h in range(2)]

        def chunk_by_lines(tiles, c):
            h, start = divmod(c * CHUNK, HALF)
            return tiles[h][:, :, start : start + CHUNK].rearrange("p t (g i) -> p g t i", i=LINE)

        sign, size = per_half("sign"), per_half("size")
        den, root, weight = {}, {}, {}
        z_bf = [keep.tile([P, CHUNK, PACK], BF16, name=f"z_bf{c}", align_bytes=ALIGN) for c in range(CHUNKS)]
        w2_codes, w2_scale = [], []

        def quantise_w2(h):
            cols = slice(h * W2_HALF, (h + 1) * W2_HALF)
            w2_codes.append(keep.tile([P, W2_HALF], U32, name=f"w2_codes{h}", tag=("picked01", "picked11")[h], align_bytes=ALIGN))
            w2_scale.append(keep.tile([P, W2_HALF], U8, name=f"w2_scale{h}", align_bytes=ALIGN))
            nc.vector.quantize_mx(w2_codes[h][:].bitcast(FP8X4), w2_scale[h][:], w2_bf[:, cols, :].rearrange("p c j -> p (c j)"))

        def within(tiles, h, planes):
            return tiles[h, planes.start // 2][:, planes.start % 2 : planes.start % 2 + len(planes), :]

        def make_denominator(h, planes):
            nc.vector.scalar_tensor_tensor(within(den, h, planes), first[h, planes][:], 0.0, within(picked, h, planes), ALU.max, ALU.add)

        def make_root(h, t):
            nc.scalar.activation(plane_of(root, h, t), plane_of(den, h, t), ACT.Abs_reciprocal_sqrt, scale=inv_idf[:, t : t + 1])

        def make_weight(h, pair, planes, cols=slice(0, HALF)):
            nc.scalar.activation(weight[h, pair][:, planes, cols], root[h, pair][:, planes, cols], ACT.Square, scale=math.sqrt(2.0))

        def make_sign(h, t, cols):
            nc.scalar.activation(sign[h][:, t, cols], plane_of(den, h, t)[:, cols], ACT.Sign, scale=idf_sign[:, t : t + 1])

        def make_size(h, planes, cols):
            nc.vector.scalar_tensor_tensor(
                size[h][:, planes.start : planes.stop, cols], first[h, planes][:, :, cols], 0.0, within(weight, h, planes)[:, :, cols], ALU.max, ALU.mult
            )

        def make_z(c, part=slice(0, CHUNK)):
            groups_of_four = slice(part.start // LINE, part.stop // LINE)
            woven = z_bf[c][:, part, :].rearrange("p (g i) t -> p g t i", i=LINE)
            nc.vector.tensor_tensor(woven, chunk_by_lines(size, c)[:, groups_of_four], chunk_by_lines(sign, c)[:, groups_of_four], ALU.mult)

        def second_product(z_codes, z_scale, blocks, bank_tag):
            bank = psum.tile([P, len(blocks), CHUNK], F32, name=bank_tag, tag=bank_tag)
            for b in blocks:
                h, start = divmod(b * P, W2_HALF)
                nc.tensor.matmul_mx(
                    bank[:, b - blocks.start, :],
                    lhsT=w2_codes[h][:, start : start + P].bitcast(FP8X4),
                    lhsT_scale=w2_scale[h][:, start : start + P],
                    rhs=z_codes[:].bitcast(FP8X4),
                    rhs_scale=z_scale[:],
                    start=True,
                    stop=True,
                )
            return bank

        exits = [
            [(range(0, 4), "second0", "den10", nc.scalar)],
            [(range(0, 4), "second1", "den11", nc.scalar)],
            [(range(0, 2), "second2", "result20", nc.scalar), (range(2, 4), "first00", "result22", nc.scalar)],
            [(range(b, b + 1), tag, f"result3{b}", (nc.vector, nc.scalar)[b % 2]) for b, tag in enumerate(("first01", "first02", "first10", "first12"))],
        ]

        def quantise_z(c, parts=(slice(0, CHUNK),)):
            z_codes = keep.tile([P, CHUNK], U32, name=f"z_codes{c}", align_bytes=ALIGN)
            z_scale = keep.tile([P, CHUNK], U8, name=f"z_scale{c}", align_bytes=ALIGN)
            for part in parts:
                nc.vector.quantize_mx(z_codes[:, part].bitcast(FP8X4), z_scale[:, part], z_bf[c][:, part, :].rearrange("p n t -> p (n t)"))
            return z_codes, z_scale

        def project(c, z_codes, z_scale):
            places = slice(c * CHUNK, (c + 1) * CHUNK)
            for blocks, bank_tag, result_tag, engine in exits[c]:
                bank = second_product(z_codes, z_scale, blocks, bank_tag)
                result = keep.tile([P, len(blocks), CHUNK], F32, name=f"result{c}{blocks.start}", tag=result_tag, align_bytes=ALIGN)
                on_vector = engine is nc.vector
                if on_vector:
                    nc.vector.tensor_copy(result[:], bank[:])
                else:
                    nc.scalar.copy(result[:], bank[:])
                queue = nc.sync if on_vector or c < CHUNKS // 2 else nc.scalar
                queue.dma_start(out_rows[:, blocks.start : blocks.stop, places], result[:])

        for h in range(2):
            for pair in range(2):
                den[h, pair] = pair_tile("den", h, pair)
                weight[h, pair] = pair_tile("weight", h, pair)
        for h, planes in groups:
            make_denominator(h, planes)

        root[0, 0] = pair_tile("root", 0, 0)
        root[0, 1] = pair_tile("root", 0, 1)
        make_root(0, 0)
        make_root(0, 1)
        make_sign(0, 0, all_places)
        make_weight(0, 0, both_planes)
        make_root(0, 2)
        make_root(0, 3)
        make_sign(0, 1, all_places)
        make_weight(0, 1, both_planes)
        make_sign(0, 2, all_places)
        make_sign(0, 3, all_places)
        root[1, 0] = keep.tile([P, 2, HALF], F32, name="root10", tag="root01", align_bytes=ALIGN)
        root[1, 1] = keep.tile([P, 2, HALF], F32, name="root11", tag="den01", align_bytes=ALIGN)
        for t in range(PACK):
            make_root(1, t)
        for cols in (low, high):
            for pair in range(2):
                make_weight(1, pair, both_planes, cols)
            for t in range(PACK):
                make_sign(1, t, cols)

        make_size(*groups[0], all_places)
        make_size(*groups[1], all_places)
        quantise_w2(0)
        quantise_w2(1)
        make_size(*groups[3], low)
        make_size(*groups[3], high)
        make_z(0)
        make_z(1)
        project(0, *quantise_z(0))
        chunk_1 = quantise_z(1)
        project(1, *chunk_1)
        warm_up(*chunk_1, "second2")
        make_size(*groups[2], low)
        make_size(*groups[4], low)
        make_z(2)
        make_size(*groups[2], high)
        make_size(*groups[4], high)
        project(2, *quantise_z(2))
        halves = (slice(0, CHUNK // 2), slice(CHUNK // 2, CHUNK))
        for part in halves:
            make_z(3, part)
        project(3, *quantise_z(3, halves))
